import numpy as np
import ml_dtypes


def mxq(x, axis, fmt="e4m3"):
    dtype, down = {"e4m3": (ml_dtypes.float8_e4m3fn, 7), "e5m2": (ml_dtypes.float8_e5m2, 14)}[fmt]
    v = np.moveaxis(np.asarray(x, np.float32).astype(ml_dtypes.bfloat16).astype(np.float64), axis, -1)
    blocks = v.reshape(v.shape[:-1] + (-1, 32))
    amax = np.abs(blocks).max(-1, keepdims=True)
    byte = np.maximum(np.where(amax > 0, np.frexp(amax)[1] - 1 + 127, 0) - down, 1)
    scale = np.exp2(byte - 127.0)
    codes = (blocks / scale).astype(np.float32).astype(dtype).astype(np.float64)
    return np.moveaxis((codes * scale).reshape(v.shape), -1, axis)


WIDE = False


def mx_kscale(k):
    if not WIDE:
        return np.ones(k)
    levels = np.array([10, -10, 5, -5, 0])
    if k % 512:
        return np.exp2(np.random.permutation(np.resize(levels, k // 32))).repeat(32)
    a = np.empty((k // 512, 16))
    for p in range(k // 512):
        a[p, :8] = np.random.permutation(np.resize(levels, 8))
        for g in range(8):
            far = levels[np.abs(levels - a[p, g]) >= 10]
            a[p, g + 8] = far[np.random.randint(len(far))]
    return np.exp2(a.ravel()).repeat(32)


def f64(x):
    return np.asarray(x).astype(np.float64)


def striped(idx):
    return np.tile(idx.reshape(-1, 16).T, (8, 1)).astype(np.uint16)


def unstriped(offs):
    return offs[:16].T.reshape(-1).astype(np.int64)


def pack_weight(w):
    k, n = w.shape
    w = f64(np.asarray(w, np.float32).astype(ml_dtypes.bfloat16)).reshape(k // 32, 32, n)
    amax = np.abs(w).max(1)
    byte = np.clip(np.where(amax > 0, np.frexp(amax)[1] - 1 + 127 - 7, 1), 1, 254)
    scaled = (w * np.exp2(127.0 - byte)[:, None, :]).reshape(k, n).astype(np.float32)
    words = np.ascontiguousarray(scaled.reshape(k // 512, 128, 4, n).transpose(0, 1, 3, 2)).astype(ml_dtypes.float8_e4m3fn).view(np.uint8)
    return words, np.ascontiguousarray(byte.astype(np.uint8).reshape(k // 512, 16, n))


def unpack_weight(words, scales):
    g, p, n, _ = words.shape
    vals = np.ascontiguousarray(words).view(ml_dtypes.float8_e4m3fn).astype(np.float64) * np.repeat(np.exp2(scales.astype(np.float64) - 127.0), 8, axis=1)[..., None]
    return vals.transpose(0, 1, 3, 2).reshape(g * 512, n)


def silu(v):
    return v / (1.0 + np.exp(-np.maximum(v, -700.0)))


K, T, S, V, H, N, J = 1024, 2048, 1024, 512, 512, 128, 512


def setup_inputs():
    n = np.random.standard_normal
    s = mx_kscale(K)[:, None]
    u = mx_kscale(H)
    r = mx_kscale(J)[:, None]
    packed_xT = pack_weight(n((K, T)) * s)
    packed_w4 = pack_weight(n((H, N)) / np.sqrt(H) / u[:, None])
    return {
        "x_words": packed_xT[0],
        "x_scales": packed_xT[1],
        "eT": (n((J, V)) * r).astype(np.float32),
        "w1": (n((K, H)) / np.sqrt(3 * K) / s * u).astype(np.float32),
        "w2": (n((K, H)) / np.sqrt(3 * K) / s * u).astype(np.float32),
        "w3": (n((J, H)) / np.sqrt(3 * J) / r * u).astype(np.float32),
        "w4_words": packed_w4[0],
        "w4_scales": packed_w4[1],
        "offs": striped(np.random.permutation(T)[:S]),
    }


def reference(x_words, x_scales, eT, w1, w2, w3, w4_words, w4_scales, offs):
    xq = unpack_weight(x_words, x_scales)[:, unstriped(offs)]
    h = silu(mxq(f64(w1), 0, "e4m3").T @ xq[:, :V] + mxq(f64(w2), 0, "e4m3").T @ xq[:, V:2 * V] + mxq(f64(w3), 0, "e4m3").T @ mxq(f64(eT), 0, "e4m3"))
    return unpack_weight(w4_words, w4_scales).T @ mxq(h, 0, "e4m3")

@@ -1,0 +1,199 @@
+from contextlib import ExitStack
+
+import concourse.mybir as mybir
+
+K, T, S, V, H, N, J = 1024, 2048, 1024, 512, 512, 128, 512
+FLOPS = 2 * (2 * K + J) * H * V + 2 * H * N * V
+
+F32 = mybir.dt.float32
+BF16 = mybir.dt.bfloat16
+I32 = mybir.dt.int32
+U32 = mybir.dt.uint32
+U16 = mybir.dt.uint16
+U8 = mybir.dt.uint8
+FP8X4 = mybir.dt.float8_e4m3fn_x4
+SILU = mybir.ActivationFunctionType.Silu
+
+P = 128
+PACK = 4
+KP = P * PACK
+VC = 128
+NC = V // VC
+
+
+def tile_picked_edgeup_silu_p_kernel(
+    tc, x_words, x_scales, eT, w1, w2, w3, w4_words, w4_scales, offs, out
+):
+    nc = tc.nc
+    with ExitStack() as ctx:
+        keep = ctx.enter_context(tc.tile_pool(name="keep", bufs=1))
+        psum = ctx.enter_context(tc.psum_pool(name="psum", bufs=1))
+
+        def sb(name, shape, dtype):
+            return keep.tile(shape, dtype, name=name, align_bytes=64)
+
+        xs_all = sb("xs_all", [P, T], U8)
+        nc.gpsimd.memset(xs_all[:].bitcast(I32), 0)
+        w4s = sb("w4s", [P, N], U8)
+        nc.gpsimd.memset(w4s[:].bitcast(I32), 0)
+        for q in range(4):
+            nc.gpsimd.dma_start(
+                w4s[32 * q : 32 * q + 4, :].bitcast(I32),
+                w4_scales[0, 4 * q : 4 * q + 4, :].bitcast(I32),
+            )
+        w4w = sb("w4w", [P, N], I32)
+        nc.gpsimd.dma_start(w4w[:], w4_words[0].rearrange("p n t -> p (n t)").bitcast(I32))
+
+        warm = sb("warm", [P, 8], F32)
+        warm2 = sb("warm2", [P, 8], F32)
+        nc.vector.memset(warm[:], 0.0)
+        nc.scalar.activation(warm2[:], warm[:], SILU)
+
+        def load_w(name, rows):
+            raw = sb(name, [P, PACK, rows.shape[1]], F32)
+            nc.sync.dma_start(raw[:], rows.rearrange("(p j) c -> p j c", j=PACK))
+            return raw
+
+        def load_x(z):
+            xw = sb(f"xw{z}", [P, T], I32)
+            nc.sync.dma_start(xw[:], x_words[z].rearrange("p n t -> p (n t)").bitcast(I32))
+            return xw
+
+        offsets = sb("offsets", [P, S // 16], U16)
+        nc.sync.dma_start(offsets[:], offs)
+        xw0 = load_x(0)
+        for q in range(4):
+            nc.sync.dma_start(
+                xs_all[32 * q : 32 * q + 8, :].bitcast(I32),
+                x_scales[:, 4 * q : 4 * q + 4, :].bitcast(I32),
+            )
+        raw_w10 = load_w("raw_w10", w1[0:KP, :])
+        xw1 = load_x(1)
+        raw_w20 = load_w("raw_w20", w2[0:KP, :])
+        raw_w11 = load_w("raw_w11", w1[KP : 2 * KP, :])
+        raw_w21 = load_w("raw_w21", w2[KP : 2 * KP, :])
+        raw_w3 = load_w("raw_w3", w3)
+        raw_e = [load_w(f"raw_e{u}", eT[:, 256 * u : 256 * (u + 1)]) for u in range(2)]
+
+        def cast_w(name, raw, m_scalar):
+            grouped = sb(name, [P, PACK * H], BF16)
+            dst = grouped[:].rearrange("p (t m j) -> p m j t", t=PACK, j=PACK)
+            src = raw[:].rearrange("p j (m t) -> p m j t", t=PACK)
+            if m_scalar > 0:
+                nc.scalar.copy(dst[:, :m_scalar], src[:, :m_scalar])
+            if m_scalar < P:
+                nc.vector.tensor_copy(dst[:, m_scalar:], src[:, m_scalar:])
+            return grouped
+
+        def quant(name, grouped, pieces):
+            width = grouped.shape[1] // PACK
+            codes = sb(name + "_c", [P, width], U32)
+            scales = sb(name + "_s", [P, width], U8)
+            step = width // pieces
+            for a in range(0, width, step):
+                nc.vector.quantize_mx(
+                    out=codes[:, a : a + step].bitcast(FP8X4),
+                    scales=scales[:, a : a + step],
+                    in_=grouped[:, PACK * a : PACK * (a + step)],
+                )
+            return codes, scales
+
+        def gather_words(z, xw):
+            g = sb(f"xg{z}", [P, S], U32)
+            nc.vector.tensor_copy(g[:], xw[:].bitcast(U32).indirect(offsets[:]))
+            return g
+
+        banks = [psum.tile([P, PACK, VC], F32, name=f"h{c}") for c in range(NC)]
+
+        def product(wq, c, codes, scales, first, last):
+            for t in range(PACK):
+                cols = slice(t * P, (t + 1) * P)
+                nc.tensor.matmul_mx(
+                    out=banks[c][:, t, :],
+                    lhsT=wq[0][:, cols].bitcast(FP8X4),
+                    lhsT_scale=wq[1][:, cols],
+                    rhs=codes.bitcast(FP8X4),
+                    rhs_scale=scales,
+                    start=first and t == 0,
+                    stop=last and t == PACK - 1,
+                )
+
+        def node_pass(wq, xg, xs, z, side, first):
+            for c in range(NC):
+                cols = slice(side * V + c * VC, side * V + (c + 1) * VC)
+                product(wq, c, xg[:, cols], xs[4 * z :, cols], first, False)
+
+        xg0 = gather_words(0, xw0)
+        xs = sb("xs", [P, S], U8)
+        nc.vector.tensor_copy(xs[:], xs_all[:].indirect(offsets[:]))
+        g10 = cast_w("g10", raw_w10, P)
+        xg1 = gather_words(1, xw1)
+        q10 = quant("q10", g10, 1)
+        node_pass(q10, xg0, xs, 0, 0, True)
+        g20 = cast_w("g20", raw_w20, 96)
+        q20 = quant("q20", g20, 1)
+        node_pass(q20, xg0, xs, 0, 1, False)
+        g11 = cast_w("g11", raw_w11, 80)
+        q11 = quant("q11", g11, 1)
+        node_pass(q11, xg1, xs, 1, 0, False)
+        g21 = cast_w("g21", raw_w21, 64)
+        q21 = quant("q21", g21, 1)
+        node_pass(q21, xg1, xs, 1, 1, False)
+        g3 = cast_w("g3", raw_w3, 44)
+        q3 = quant("q3", g3, 2)
+
+        def cast_e(c, copy):
+            grouped = sb(f"ge{c}", [P, PACK * VC], BF16)
+            raw = raw_e[c // 2]
+            a = (c % 2) * VC
+            copy(
+                grouped[:].rearrange("p (g i j) -> p g j i", i=4, j=PACK),
+                raw[:, :, a : a + VC].rearrange("p j (g i) -> p g j i", i=4),
+            )
+            return grouped
+
+        def first_layer(c, ge):
+            qe = quant(f"qe{c}", ge, 1)
+            product(q3, c, qe[0][:], qe[1][:], False, True)
+            hb = sb(f"hb{c}", [P, PACK * VC], BF16)
+            nc.scalar.activation(
+                hb[:].rearrange("p (v t) -> p v t", t=PACK),
+                banks[c][:].rearrange("p t v -> p v t"),
+                SILU,
+            )
+            return hb
+
+        def second_layer(c, hb):
+            qh = quant(f"qh{c}", hb, 1)
+            acc = psum.tile([P, VC], F32, name=f"o{c}")
+            nc.tensor.matmul_mx(
+                out=acc[:],
+                lhsT=w4w[:].bitcast(FP8X4),
+                lhsT_scale=w4s[:],
+                rhs=qh[0][:].bitcast(FP8X4),
+                rhs_scale=qh[1][:],
+                start=True,
+                stop=True,
+            )
+            return acc
+
+        def way_out(c, acc):
+            res = sb(f"res{c}", [P, VC], F32)
+            nc.vector.tensor_copy(res[:], acc[:])
+            nc.sync.dma_start(out[:, c * VC : (c + 1) * VC], res[:])
+
+        ge0 = cast_e(0, nc.scalar.copy)
+        ge1 = cast_e(1, nc.vector.tensor_copy)
+        hb0 = first_layer(0, ge0)
+        hb1 = first_layer(1, ge1)
+        ge2 = cast_e(2, nc.vector.tensor_copy)
+        ge3 = cast_e(3, nc.vector.tensor_copy)
+        hb2 = first_layer(2, ge2)
+        hb3 = first_layer(3, ge3)
+        hbs = [hb0, hb1, hb2, hb3]
+        accs = []
+        for c in range(NC):
+            accs.append(second_layer(c, hbs[c]))
+            if c > 0:
+                way_out(c - 1, accs[c - 1])
+        way_out(NC - 1, accs[NC - 1])

@@ -35,21 +35,13 @@ def tile_picked_edgeup_silu_p_kernel(
         xs_all = sb("xs_all", [P, T], U8)
         nc.gpsimd.memset(xs_all[:].bitcast(I32), 0)
         w4s = sb("w4s", [P, N], U8)
-        nc.gpsimd.memset(w4s[:].bitcast(I32), 0)
-        for q in range(4):
-            nc.gpsimd.dma_start(
-                w4s[32 * q : 32 * q + 4, :].bitcast(I32),
-                w4_scales[0, 4 * q : 4 * q + 4, :].bitcast(I32),
-            )
-        w4w = sb("w4w", [P, N], I32)
-        nc.gpsimd.dma_start(w4w[:], w4_words[0].rearrange("p n t -> p (n t)").bitcast(I32))
-
+        nc.vector.memset(w4s[:].bitcast(I32), 0)
         warm = sb("warm", [P, 8], F32)
         warm2 = sb("warm2", [P, 8], F32)
         nc.vector.memset(warm[:], 0.0)
         nc.scalar.activation(warm2[:], warm[:], SILU)
 
-        def load_w(name, rows):
+        def load_rows(name, rows):
             raw = sb(name, [P, PACK, rows.shape[1]], F32)
             nc.sync.dma_start(raw[:], rows.rearrange("(p j) c -> p j c", j=PACK))
             return raw
@@ -67,36 +59,47 @@ def tile_picked_edgeup_silu_p_kernel(
                 xs_all[32 * q : 32 * q + 8, :].bitcast(I32),
                 x_scales[:, 4 * q : 4 * q + 4, :].bitcast(I32),
             )
-        raw_w10 = load_w("raw_w10", w1[0:KP, :])
+        raw_w10 = load_rows("raw_w10", w1[0:KP, :])
         xw1 = load_x(1)
-        raw_w20 = load_w("raw_w20", w2[0:KP, :])
-        raw_w11 = load_w("raw_w11", w1[KP : 2 * KP, :])
-        raw_w21 = load_w("raw_w21", w2[KP : 2 * KP, :])
-        raw_w3 = load_w("raw_w3", w3)
-        raw_e = [load_w(f"raw_e{u}", eT[:, 256 * u : 256 * (u + 1)]) for u in range(2)]
+        raw_w20 = load_rows("raw_w20", w2[0:KP, :])
+        raw_w11 = load_rows("raw_w11", w1[KP : 2 * KP, :])
+        raw_w21 = load_rows("raw_w21", w2[KP : 2 * KP, :])
+        raw_w3 = [load_rows(f"raw_w3{u}", w3[:, 256 * u : 256 * (u + 1)]) for u in range(2)]
+        raw_e = [load_rows(f"raw_e{c}", eT[:, VC * c : VC * (c + 1)]) for c in range(NC)]
+        w4w = sb("w4w", [P, N], I32)
+        nc.sync.dma_start(w4w[:], w4_words[0].rearrange("p n t -> p (n t)").bitcast(I32))
+        for q in range(4):
+            nc.sync.dma_start(
+                w4s[32 * q : 32 * q + 4, :].bitcast(I32),
+                w4_scales[0, 4 * q : 4 * q + 4, :].bitcast(I32),
+            )
 
         def cast_w(name, raw, m_scalar):
-            grouped = sb(name, [P, PACK * H], BF16)
-            dst = grouped[:].rearrange("p (t m j) -> p m j t", t=PACK, j=PACK)
-            src = raw[:].rearrange("p j (m t) -> p m j t", t=PACK)
+            ms = raw.shape[2] // PACK
+            grouped = sb(name, [P, PACK * raw.shape[2]], BF16)
+            dst = grouped[:].rearrange("p (u e m j) -> p u m j e", u=2, e=2, j=PACK)
+            src = raw[:].rearrange("p j (m u e) -> p u m j e", u=2, e=2)
             if m_scalar > 0:
-                nc.scalar.copy(dst[:, :m_scalar], src[:, :m_scalar])
-            if m_scalar < P:
-                nc.vector.tensor_copy(dst[:, m_scalar:], src[:, m_scalar:])
+                nc.scalar.copy(dst[:, :, :m_scalar], src[:, :, :m_scalar])
+            if m_scalar < ms:
+                nc.vector.tensor_copy(dst[:, :, m_scalar:], src[:, :, m_scalar:])
             return grouped
 
-        def quant(name, grouped, pieces):
+        def planes(name, width):
+            return sb(name + "_c", [P, width], U32), sb(name + "_s", [P, width], U8)
+
+        def quant_into(q, a, grouped):
             width = grouped.shape[1] // PACK
-            codes = sb(name + "_c", [P, width], U32)
-            scales = sb(name + "_s", [P, width], U8)
-            step = width // pieces
-            for a in range(0, width, step):
-                nc.vector.quantize_mx(
-                    out=codes[:, a : a + step].bitcast(FP8X4),
-                    scales=scales[:, a : a + step],
-                    in_=grouped[:, PACK * a : PACK * (a + step)],
-                )
-            return codes, scales
+            nc.vector.quantize_mx(
+                out=q[0][:, a : a + width].bitcast(FP8X4),
+                scales=q[1][:, a : a + width],
+                in_=grouped,
+            )
+
+        def quant(name, grouped):
+            q = planes(name, grouped.shape[1] // PACK)
+            quant_into(q, 0, grouped[:])
+            return q
 
         def gather_words(z, xw):
             g = sb(f"xg{z}", [P, S], U32)
@@ -126,34 +129,34 @@ def tile_picked_edgeup_silu_p_kernel(
         xg0 = gather_words(0, xw0)
         xs = sb("xs", [P, S], U8)
         nc.vector.tensor_copy(xs[:], xs_all[:].indirect(offsets[:]))
-        g10 = cast_w("g10", raw_w10, P)
+        g10 = cast_w("g10", raw_w10, 128)
         xg1 = gather_words(1, xw1)
-        q10 = quant("q10", g10, 1)
+        q10 = quant("q10", g10)
         node_pass(q10, xg0, xs, 0, 0, True)
         g20 = cast_w("g20", raw_w20, 96)
-        q20 = quant("q20", g20, 1)
+        q20 = quant("q20", g20)
         node_pass(q20, xg0, xs, 0, 1, False)
         g11 = cast_w("g11", raw_w11, 80)
-        q11 = quant("q11", g11, 1)
+        q11 = quant("q11", g11)
         node_pass(q11, xg1, xs, 1, 0, False)
-        g21 = cast_w("g21", raw_w21, 64)
-        q21 = quant("q21", g21, 1)
+        g21 = cast_w("g21", raw_w21, 44)
+        q21 = quant("q21", g21)
         node_pass(q21, xg1, xs, 1, 1, False)
-        g3 = cast_w("g3", raw_w3, 44)
-        q3 = quant("q3", g3, 2)
+        q3 = planes("q3", H)
+        for u in range(2):
+            g3 = cast_w(f"g3{u}", raw_w3[u], (40, 22)[u])
+            for t in range(PACK):
+                quant_into(q3, t * P + 64 * u, g3[:, 256 * t : 256 * (t + 1)])
 
         def cast_e(c, copy):
             grouped = sb(f"ge{c}", [P, PACK * VC], BF16)
-            raw = raw_e[c // 2]
-            a = (c % 2) * VC
             copy(
                 grouped[:].rearrange("p (g i j) -> p g j i", i=4, j=PACK),
-                raw[:, :, a : a + VC].rearrange("p j (g i) -> p g j i", i=4),
+                raw_e[c][:].rearrange("p j (g i) -> p g j i", i=4),
             )
             return grouped
 
-        def first_layer(c, ge):
-            qe = quant(f"qe{c}", ge, 1)
+        def first_layer(c, qe):
             product(q3, c, qe[0][:], qe[1][:], False, True)
             hb = sb(f"hb{c}", [P, PACK * VC], BF16)
             nc.scalar.activation(
@@ -164,7 +167,7 @@ def tile_picked_edgeup_silu_p_kernel(
             return hb
 
         def second_layer(c, hb):
-            qh = quant(f"qh{c}", hb, 1)
+            qh = quant(f"qh{c}", hb)
             acc = psum.tile([P, VC], F32, name=f"o{c}")
             nc.tensor.matmul_mx(
                 out=acc[:],
@@ -183,17 +186,18 @@ def tile_picked_edgeup_silu_p_kernel(
             nc.sync.dma_start(out[:, c * VC : (c + 1) * VC], res[:])
 
         ge0 = cast_e(0, nc.scalar.copy)
-        ge1 = cast_e(1, nc.vector.tensor_copy)
-        hb0 = first_layer(0, ge0)
-        hb1 = first_layer(1, ge1)
+        ge1 = cast_e(1, nc.scalar.copy)
+        hb0 = first_layer(0, quant("qe0", ge0))
         ge2 = cast_e(2, nc.vector.tensor_copy)
+        hb1 = first_layer(1, quant("qe1", ge1))
+        hb2 = first_layer(2, quant("qe2", ge2))
         ge3 = cast_e(3, nc.vector.tensor_copy)
-        hb2 = first_layer(2, ge2)
-        hb3 = first_layer(3, ge3)
-        hbs = [hb0, hb1, hb2, hb3]
-        accs = []
-        for c in range(NC):
-            accs.append(second_layer(c, hbs[c]))
-            if c > 0:
-                way_out(c - 1, accs[c - 1])
-        way_out(NC - 1, accs[NC - 1])
+        acc0 = second_layer(0, hb0)
+        hb3 = first_layer(3, quant("qe3", ge3))
+        acc1 = second_layer(1, hb1)
+        way_out(0, acc0)
+        acc2 = second_layer(2, hb2)
+        way_out(1, acc1)
+        way_out(2, acc2)
+        acc3 = second_layer(3, hb3)
+        way_out(3, acc3)

@@ -51,9 +51,9 @@ def tile_picked_edgeup_silu_p_kernel(
             nc.sync.dma_start(xw[:], x_words[z].rearrange("p n t -> p (n t)").bitcast(I32))
             return xw
 
+        xw0 = load_x(0)
         offsets = sb("offsets", [P, S // 16], U16)
         nc.sync.dma_start(offsets[:], offs)
-        xw0 = load_x(0)
         for q in range(4):
             nc.sync.dma_start(
                 xs_all[32 * q : 32 * q + 8, :].bitcast(I32),
@@ -64,8 +64,8 @@ def tile_picked_edgeup_silu_p_kernel(
         raw_w20 = load_rows("raw_w20", w2[0:KP, :])
         raw_w11 = load_rows("raw_w11", w1[KP : 2 * KP, :])
         raw_w21 = load_rows("raw_w21", w2[KP : 2 * KP, :])
-        raw_w3 = [load_rows(f"raw_w3{u}", w3[:, 256 * u : 256 * (u + 1)]) for u in range(2)]
-        raw_e = [load_rows(f"raw_e{c}", eT[:, VC * c : VC * (c + 1)]) for c in range(NC)]
+        raw_w3 = load_rows("raw_w3", w3)
+        raw_e = [load_rows(f"raw_e{u}", eT[:, 2 * VC * u : 2 * VC * (u + 1)]) for u in range(2)]
         w4w = sb("w4w", [P, N], I32)
         nc.sync.dma_start(w4w[:], w4_words[0].rearrange("p n t -> p (n t)").bitcast(I32))
         for q in range(4):
@@ -143,16 +143,15 @@ def tile_picked_edgeup_silu_p_kernel(
         q21 = quant("q21", g21)
         node_pass(q21, xg1, xs, 1, 1, False)
         q3 = planes("q3", H)
-        for u in range(2):
-            g3 = cast_w(f"g3{u}", raw_w3[u], (40, 22)[u])
-            for t in range(PACK):
-                quant_into(q3, t * P + 64 * u, g3[:, 256 * t : 256 * (t + 1)])
+        g3 = cast_w("g3", raw_w3, 44)
+        for a in range(0, H, 2 * P):
+            quant_into(q3, a, g3[:, PACK * a : PACK * (a + 2 * P)])
 
         def cast_e(c, copy):
             grouped = sb(f"ge{c}", [P, PACK * VC], BF16)
             copy(
                 grouped[:].rearrange("p (g i j) -> p g j i", i=4, j=PACK),
-                raw_e[c][:].rearrange("p j (g i) -> p g j i", i=4),
+                raw_e[c // 2][:, :, (c % 2) * VC : (c % 2 + 1) * VC].rearrange("p j (g i) -> p g j i", i=4),
             )
             return grouped
 
@@ -186,7 +185,7 @@ def tile_picked_edgeup_silu_p_kernel(
             nc.sync.dma_start(out[:, c * VC : (c + 1) * VC], res[:])
 
         ge0 = cast_e(0, nc.scalar.copy)
-        ge1 = cast_e(1, nc.scalar.copy)
+        ge1 = cast_e(1, nc.vector.tensor_copy)
         hb0 = first_layer(0, quant("qe0", ge0))
         ge2 = cast_e(2, nc.vector.tensor_copy)
         hb1 = first_layer(1, quant("qe1", ge1))

@@ -16,9 +16,15 @@ SILU = mybir.ActivationFunctionType.Silu
 
 P = 128
 PACK = 4
-KP = P * PACK
-VC = 128
-NC = V // VC
+K_PASS = P * PACK
+QUADRANT = 32
+SCALE_ROWS = 4
+CHUNK = 128
+CHUNKS = V // CHUNK
+
+SCALAR_SHARE_W1 = (128, 80)
+SCALAR_SHARE_W2 = (96, 44)
+SCALAR_SHARE_W3 = 96
 
 
 def tile_picked_edgeup_silu_p_kernel(
@@ -36,167 +42,161 @@ def tile_picked_edgeup_silu_p_kernel(
         nc.gpsimd.memset(xs_all[:].bitcast(I32), 0)
         w4s = sb("w4s", [P, N], U8)
         nc.vector.memset(w4s[:].bitcast(I32), 0)
-        warm = sb("warm", [P, 8], F32)
-        warm2 = sb("warm2", [P, 8], F32)
-        nc.vector.memset(warm[:], 0.0)
-        nc.scalar.activation(warm2[:], warm[:], SILU)
 
         def load_rows(name, rows):
             raw = sb(name, [P, PACK, rows.shape[1]], F32)
             nc.sync.dma_start(raw[:], rows.rearrange("(p j) c -> p j c", j=PACK))
             return raw
 
-        def load_x(z):
-            xw = sb(f"xw{z}", [P, T], I32)
-            nc.sync.dma_start(xw[:], x_words[z].rearrange("p n t -> p (n t)").bitcast(I32))
-            return xw
+        def load_words(name, words):
+            tile = sb(name, [P, words.shape[1]], I32)
+            nc.sync.dma_start(tile[:], words.rearrange("p n t -> p (n t)").bitcast(I32))
+            return tile
 
-        xw0 = load_x(0)
+        xw0 = load_words("xw0", x_words[0])
         offsets = sb("offsets", [P, S // 16], U16)
         nc.sync.dma_start(offsets[:], offs)
-        for q in range(4):
+        for q in (0, 2, 1, 3):
             nc.sync.dma_start(
-                xs_all[32 * q : 32 * q + 8, :].bitcast(I32),
-                x_scales[:, 4 * q : 4 * q + 4, :].bitcast(I32),
+                xs_all[QUADRANT * q : QUADRANT * q + 2 * SCALE_ROWS, :].bitcast(I32),
+                x_scales[:, SCALE_ROWS * q : SCALE_ROWS * (q + 1), :].bitcast(I32),
             )
-        raw_w10 = load_rows("raw_w10", w1[0:KP, :])
-        xw1 = load_x(1)
-        raw_w20 = load_rows("raw_w20", w2[0:KP, :])
-        raw_w11 = load_rows("raw_w11", w1[KP : 2 * KP, :])
-        raw_w21 = load_rows("raw_w21", w2[KP : 2 * KP, :])
+        raw_w10 = load_rows("raw_w10", w1[0:K_PASS, :])
+        xw1 = load_words("xw1", x_words[1])
+        raw_w20 = load_rows("raw_w20", w2[0:K_PASS, :])
+        raw_w11 = load_rows("raw_w11", w1[K_PASS:K, :])
+        raw_w21 = load_rows("raw_w21", w2[K_PASS:K, :])
         raw_w3 = load_rows("raw_w3", w3)
-        raw_e = [load_rows(f"raw_e{u}", eT[:, 2 * VC * u : 2 * VC * (u + 1)]) for u in range(2)]
-        w4w = sb("w4w", [P, N], I32)
-        nc.sync.dma_start(w4w[:], w4_words[0].rearrange("p n t -> p (n t)").bitcast(I32))
+        raw_e = [load_rows(f"raw_e{u}", eT[:, 2 * CHUNK * u : 2 * CHUNK * (u + 1)]) for u in range(2)]
+        w4w = load_words("w4w", w4_words[0])
         for q in range(4):
             nc.sync.dma_start(
-                w4s[32 * q : 32 * q + 4, :].bitcast(I32),
-                w4_scales[0, 4 * q : 4 * q + 4, :].bitcast(I32),
+                w4s[QUADRANT * q : QUADRANT * q + SCALE_ROWS, :].bitcast(I32),
+                w4_scales[0, SCALE_ROWS * q : SCALE_ROWS * (q + 1), :].bitcast(I32),
             )
 
-        def cast_w(name, raw, m_scalar):
-            ms = raw.shape[2] // PACK
-            grouped = sb(name, [P, PACK * raw.shape[2]], BF16)
-            dst = grouped[:].rearrange("p (u e m j) -> p u m j e", u=2, e=2, j=PACK)
+        def cast_weights(name, raw, m_scalar):
+            dealt = sb(name, [P, PACK * H], BF16)
+            dst = dealt[:].rearrange("p (u e m j) -> p u m j e", u=2, e=2, j=PACK)
             src = raw[:].rearrange("p j (m u e) -> p u m j e", u=2, e=2)
-            if m_scalar > 0:
-                nc.scalar.copy(dst[:, :, :m_scalar], src[:, :, :m_scalar])
-            if m_scalar < ms:
+            nc.scalar.copy(dst[:, :, :m_scalar], src[:, :, :m_scalar])
+            if m_scalar < P:
                 nc.vector.tensor_copy(dst[:, :, m_scalar:], src[:, :, m_scalar:])
-            return grouped
+            return dealt
 
-        def planes(name, width):
+        def operand(name, width):
             return sb(name + "_c", [P, width], U32), sb(name + "_s", [P, width], U8)
 
-        def quant_into(q, a, grouped):
-            width = grouped.shape[1] // PACK
+        def quantise_into(mx, first, values):
+            width = values.shape[1] // PACK
             nc.vector.quantize_mx(
-                out=q[0][:, a : a + width].bitcast(FP8X4),
-                scales=q[1][:, a : a + width],
-                in_=grouped,
+                out=mx[0][:, first : first + width].bitcast(FP8X4),
+                scales=mx[1][:, first : first + width],
+                in_=values,
             )
 
-        def quant(name, grouped):
-            q = planes(name, grouped.shape[1] // PACK)
-            quant_into(q, 0, grouped[:])
-            return q
+        def quantise(name, values):
+            mx = operand(name, values.shape[1] // PACK)
+            quantise_into(mx, 0, values[:])
+            return mx
 
-        def gather_words(z, xw):
-            g = sb(f"xg{z}", [P, S], U32)
-            nc.vector.tensor_copy(g[:], xw[:].bitcast(U32).indirect(offsets[:]))
-            return g
+        def gather_words(name, table):
+            picked = sb(name, [P, S], U32)
+            nc.vector.tensor_copy(picked[:], table[:].bitcast(U32).indirect(offsets[:]))
+            return picked
 
-        banks = [psum.tile([P, PACK, VC], F32, name=f"h{c}") for c in range(NC)]
+        banks = [psum.tile([P, PACK, CHUNK], F32, name=f"h{c}") for c in range(CHUNKS)]
 
-        def product(wq, c, codes, scales, first, last):
+        def chunk_pass(weights, c, words, scales, opens, closes):
             for t in range(PACK):
                 cols = slice(t * P, (t + 1) * P)
                 nc.tensor.matmul_mx(
                     out=banks[c][:, t, :],
-                    lhsT=wq[0][:, cols].bitcast(FP8X4),
-                    lhsT_scale=wq[1][:, cols],
-                    rhs=codes.bitcast(FP8X4),
+                    lhsT=weights[0][:, cols].bitcast(FP8X4),
+                    lhsT_scale=weights[1][:, cols],
+                    rhs=words.bitcast(FP8X4),
                     rhs_scale=scales,
-                    start=first and t == 0,
-                    stop=last and t == PACK - 1,
+                    start=opens and t == 0,
+                    stop=closes and t == PACK - 1,
                 )
 
-        def node_pass(wq, xg, xs, z, side, first):
-            for c in range(NC):
-                cols = slice(side * V + c * VC, side * V + (c + 1) * VC)
-                product(wq, c, xg[:, cols], xs[4 * z :, cols], first, False)
+        def node_pass(weights, words, scales, z, side, opens):
+            for c in range(CHUNKS):
+                cols = slice(side * V + c * CHUNK, side * V + (c + 1) * CHUNK)
+                chunk_pass(weights, c, words[:, cols], scales[SCALE_ROWS * z :, cols], opens, False)
 
-        xg0 = gather_words(0, xw0)
+        xg0 = gather_words("xg0", xw0)
         xs = sb("xs", [P, S], U8)
         nc.vector.tensor_copy(xs[:], xs_all[:].indirect(offsets[:]))
-        g10 = cast_w("g10", raw_w10, 128)
-        xg1 = gather_words(1, xw1)
-        q10 = quant("q10", g10)
-        node_pass(q10, xg0, xs, 0, 0, True)
-        g20 = cast_w("g20", raw_w20, 96)
-        q20 = quant("q20", g20)
-        node_pass(q20, xg0, xs, 0, 1, False)
-        g11 = cast_w("g11", raw_w11, 80)
-        q11 = quant("q11", g11)
-        node_pass(q11, xg1, xs, 1, 0, False)
-        g21 = cast_w("g21", raw_w21, 44)
-        q21 = quant("q21", g21)
-        node_pass(q21, xg1, xs, 1, 1, False)
-        q3 = planes("q3", H)
-        g3 = cast_w("g3", raw_w3, 44)
-        for a in range(0, H, 2 * P):
-            quant_into(q3, a, g3[:, PACK * a : PACK * (a + 2 * P)])
+        dealt_w10 = cast_weights("g10", raw_w10, SCALAR_SHARE_W1[0])
+        xg1 = gather_words("xg1", xw1)
+        node_pass(quantise("q10", dealt_w10), xg0, xs, 0, 0, True)
+        node_pass(quantise("q20", cast_weights("g20", raw_w20, SCALAR_SHARE_W2[0])), xg0, xs, 0, 1, False)
+        node_pass(quantise("q11", cast_weights("g11", raw_w11, SCALAR_SHARE_W1[1])), xg1, xs, 1, 0, False)
+        node_pass(quantise("q21", cast_weights("g21", raw_w21, SCALAR_SHARE_W2[1])), xg1, xs, 1, 1, False)
 
-        def cast_e(c, copy):
-            grouped = sb(f"ge{c}", [P, PACK * VC], BF16)
-            copy(
-                grouped[:].rearrange("p (g i j) -> p g j i", i=4, j=PACK),
-                raw_e[c // 2][:, :, (c % 2) * VC : (c % 2 + 1) * VC].rearrange("p j (g i) -> p g j i", i=4),
+        q3 = operand("q3", H)
+        src3 = raw_w3[:].rearrange("p j (m u e) -> p u m j e", u=2, e=2)
+        dealt_w3 = [sb(f"g3{u}", [P, 2 * H], BF16) for u in range(2)]
+        dst3 = [pair[:].rearrange("p (e m j) -> p m j e", e=2, j=PACK) for pair in dealt_w3]
+        nc.scalar.copy(dst3[0][:, :SCALAR_SHARE_W3], src3[:, 0, :SCALAR_SHARE_W3])
+        nc.vector.tensor_copy(dst3[1], src3[:, 1])
+        nc.vector.tensor_copy(dst3[0][:, SCALAR_SHARE_W3:], src3[:, 0, SCALAR_SHARE_W3:])
+        quantise_into(q3, 2 * P, dealt_w3[1][:])
+        quantise_into(q3, 0, dealt_w3[0][:])
+
+        def cast_edges(c):
+            values = sb(f"ge{c}", [P, PACK * CHUNK], BF16)
+            first = (c % 2) * CHUNK
+            nc.vector.tensor_copy(
+                values[:].rearrange("p (g i j) -> p g j i", i=4, j=PACK),
+                raw_e[c // 2][:, :, first : first + CHUNK].rearrange("p j (g i) -> p g j i", i=4),
             )
-            return grouped
+            return values
 
-        def first_layer(c, qe):
-            product(q3, c, qe[0][:], qe[1][:], False, True)
-            hb = sb(f"hb{c}", [P, PACK * VC], BF16)
+        def first_layer(c, edge_values):
+            words, scales = quantise(f"qe{c}", edge_values)
+            chunk_pass(q3, c, words[:], scales[:], False, True)
+            hidden = sb(f"hb{c}", [P, PACK * CHUNK], BF16)
             nc.scalar.activation(
-                hb[:].rearrange("p (v t) -> p v t", t=PACK),
+                hidden[:].rearrange("p (v t) -> p v t", t=PACK),
                 banks[c][:].rearrange("p t v -> p v t"),
                 SILU,
             )
-            return hb
+            return hidden
 
-        def second_layer(c, hb):
-            qh = quant(f"qh{c}", hb)
-            acc = psum.tile([P, VC], F32, name=f"o{c}")
+        results = [psum.tile([P, CHUNK], F32, name=f"o{c}") for c in range(CHUNKS)]
+
+        def second_layer(c, hidden):
+            words, scales = quantise(f"qh{c}", hidden)
             nc.tensor.matmul_mx(
-                out=acc[:],
+                out=results[c][:],
                 lhsT=w4w[:].bitcast(FP8X4),
                 lhsT_scale=w4s[:],
-                rhs=qh[0][:].bitcast(FP8X4),
-                rhs_scale=qh[1][:],
+                rhs=words[:].bitcast(FP8X4),
+                rhs_scale=scales[:],
                 start=True,
                 stop=True,
             )
-            return acc
 
-        def way_out(c, acc):
-            res = sb(f"res{c}", [P, VC], F32)
-            nc.vector.tensor_copy(res[:], acc[:])
-            nc.sync.dma_start(out[:, c * VC : (c + 1) * VC], res[:])
+        def store(c):
+            staged = sb(f"res{c}", [P, CHUNK], F32)
+            nc.vector.tensor_copy(staged[:], results[c][:])
+            nc.sync.dma_start(out[:, c * CHUNK : (c + 1) * CHUNK], staged[:])
 
-        ge0 = cast_e(0, nc.scalar.copy)
-        ge1 = cast_e(1, nc.vector.tensor_copy)
-        hb0 = first_layer(0, quant("qe0", ge0))
-        ge2 = cast_e(2, nc.vector.tensor_copy)
-        hb1 = first_layer(1, quant("qe1", ge1))
-        hb2 = first_layer(2, quant("qe2", ge2))
-        ge3 = cast_e(3, nc.vector.tensor_copy)
-        acc0 = second_layer(0, hb0)
-        hb3 = first_layer(3, quant("qe3", ge3))
-        acc1 = second_layer(1, hb1)
-        way_out(0, acc0)
-        acc2 = second_layer(2, hb2)
-        way_out(1, acc1)
-        way_out(2, acc2)
-        acc3 = second_layer(3, hb3)
-        way_out(3, acc3)
+        edges0 = cast_edges(0)
+        edges1 = cast_edges(1)
+        hidden0 = first_layer(0, edges0)
+        edges2 = cast_edges(2)
+        hidden1 = first_layer(1, edges1)
+        hidden2 = first_layer(2, edges2)
+        edges3 = cast_edges(3)
+        second_layer(0, hidden0)
+        hidden3 = first_layer(3, edges3)
+        second_layer(1, hidden1)
+        store(0)
+        second_layer(2, hidden2)
+        store(1)
+        store(2)
+        second_layer(3, hidden3)
+        store(3)

@@ -24,7 +24,7 @@ CHUNKS = V // CHUNK
 
 SCALAR_SHARE_W1 = (128, 80)
 SCALAR_SHARE_W2 = (96, 44)
-SCALAR_SHARE_W3 = 96
+EDGE_LOADS = ((0, 2), (2, 1), (3, 1))
 
 
 def tile_picked_edgeup_silu_p_kernel(
@@ -67,7 +67,10 @@ def tile_picked_edgeup_silu_p_kernel(
         raw_w11 = load_rows("raw_w11", w1[K_PASS:K, :])
         raw_w21 = load_rows("raw_w21", w2[K_PASS:K, :])
         raw_w3 = load_rows("raw_w3", w3)
-        raw_e = [load_rows(f"raw_e{u}", eT[:, 2 * CHUNK * u : 2 * CHUNK * (u + 1)]) for u in range(2)]
+        raw_e = []
+        for first, count in EDGE_LOADS:
+            raw = load_rows(f"raw_e{first}", eT[:, first * CHUNK : (first + count) * CHUNK])
+            raw_e.extend(raw[:, :, i * CHUNK : (i + 1) * CHUNK] for i in range(count))
         w4w = load_words("w4w", w4_words[0])
         for q in range(4):
             nc.sync.dma_start(
@@ -128,6 +131,8 @@ def tile_picked_edgeup_silu_p_kernel(
         xg0 = gather_words("xg0", xw0)
         xs = sb("xs", [P, S], U8)
         nc.vector.tensor_copy(xs[:], xs_all[:].indirect(offsets[:]))
+        unread = sb("unread", [P, 1], F32)
+        nc.scalar.activation(unread[:], raw_w10[:, 0, 0:1], SILU)
         dealt_w10 = cast_weights("g10", raw_w10, SCALAR_SHARE_W1[0])
         xg1 = gather_words("xg1", xw1)
         node_pass(quantise("q10", dealt_w10), xg0, xs, 0, 0, True)
@@ -139,18 +144,16 @@ def tile_picked_edgeup_silu_p_kernel(
         src3 = raw_w3[:].rearrange("p j (m u e) -> p u m j e", u=2, e=2)
         dealt_w3 = [sb(f"g3{u}", [P, 2 * H], BF16) for u in range(2)]
         dst3 = [pair[:].rearrange("p (e m j) -> p m j e", e=2, j=PACK) for pair in dealt_w3]
-        nc.scalar.copy(dst3[0][:, :SCALAR_SHARE_W3], src3[:, 0, :SCALAR_SHARE_W3])
+        nc.scalar.copy(dst3[0], src3[:, 0])
         nc.vector.tensor_copy(dst3[1], src3[:, 1])
-        nc.vector.tensor_copy(dst3[0][:, SCALAR_SHARE_W3:], src3[:, 0, SCALAR_SHARE_W3:])
         quantise_into(q3, 2 * P, dealt_w3[1][:])
-        quantise_into(q3, 0, dealt_w3[0][:])
 
         def cast_edges(c):
             values = sb(f"ge{c}", [P, PACK * CHUNK], BF16)
-            first = (c % 2) * CHUNK
-            nc.vector.tensor_copy(
+            copy = nc.scalar.copy if c == 1 else nc.vector.tensor_copy
+            copy(
                 values[:].rearrange("p (g i j) -> p g j i", i=4, j=PACK),
-                raw_e[c // 2][:, :, first : first + CHUNK].rearrange("p j (g i) -> p g j i", i=4),
+                raw_e[c].rearrange("p j (g i) -> p g j i", i=4),
             )
             return values
 
@@ -184,19 +187,15 @@ def tile_picked_edgeup_silu_p_kernel(
             nc.vector.tensor_copy(staged[:], results[c][:])
             nc.sync.dma_start(out[:, c * CHUNK : (c + 1) * CHUNK], staged[:])
 
-        edges0 = cast_edges(0)
-        edges1 = cast_edges(1)
-        hidden0 = first_layer(0, edges0)
-        edges2 = cast_edges(2)
-        hidden1 = first_layer(1, edges1)
-        hidden2 = first_layer(2, edges2)
-        edges3 = cast_edges(3)
-        second_layer(0, hidden0)
-        hidden3 = first_layer(3, edges3)
-        second_layer(1, hidden1)
-        store(0)
-        second_layer(2, hidden2)
-        store(1)
-        store(2)
-        second_layer(3, hidden3)
-        store(3)
+        values = [cast_edges(0), cast_edges(1)]
+        quantise_into(q3, 0, dealt_w3[0][:])
+        hidden = [first_layer(0, values[0])]
+        values.append(cast_edges(2))
+        hidden.append(first_layer(1, values[1]))
+        hidden.append(first_layer(2, values[2]))
+        hidden.append(first_layer(3, cast_edges(3)))
+        second_layer(0, hidden[0])
+        for c in range(1, CHUNKS):
+            second_layer(c, hidden[c])
+            store(c - 1)
+        store(CHUNKS - 1)

@@ -56,12 +56,18 @@ def tile_picked_edgeup_silu_p_kernel(
         xw0 = load_words("xw0", x_words[0])
         offsets = sb("offsets", [P, S // 16], U16)
         nc.sync.dma_start(offsets[:], offs)
-        for q in (0, 2, 1, 3):
-            nc.sync.dma_start(
-                xs_all[QUADRANT * q : QUADRANT * q + 2 * SCALE_ROWS, :].bitcast(I32),
-                x_scales[:, SCALE_ROWS * q : SCALE_ROWS * (q + 1), :].bitcast(I32),
-            )
+        def load_scale_rows(r):
+            for z in range(2):
+                nc.sync.dma_start(
+                    xs_all[SCALE_ROWS * z + r : P : QUADRANT, :].bitcast(I32),
+                    x_scales[z, r : 16 : SCALE_ROWS, :].bitcast(I32),
+                )
+
+        load_scale_rows(0)
+        load_scale_rows(1)
         raw_w10 = load_rows("raw_w10", w1[0:K_PASS, :])
+        load_scale_rows(2)
+        load_scale_rows(3)
         xw1 = load_words("xw1", x_words[1])
         raw_w20 = load_rows("raw_w20", w2[0:K_PASS, :])
         raw_w11 = load_rows("raw_w11", w1[K_PASS:K, :])

@@ -23,7 +23,7 @@ CHUNK = 128
 CHUNKS = V // CHUNK
 
 SCALAR_SHARE_W1 = (128, 80)
-SCALAR_SHARE_W2 = (96, 44)
+SCALAR_SHARE_W2 = (96, 72)
 EDGE_LOADS = ((0, 2), (2, 1), (3, 1))
 
 
@@ -58,10 +58,13 @@ def tile_picked_edgeup_silu_p_kernel(
         nc.sync.dma_start(offsets[:], offs)
         def load_scale_rows(r):
             for z in range(2):
-                nc.sync.dma_start(
-                    xs_all[SCALE_ROWS * z + r : P : QUADRANT, :].bitcast(I32),
-                    x_scales[z, r : 16 : SCALE_ROWS, :].bitcast(I32),
-                )
+                rows = xs_all[SCALE_ROWS * z + r : P : QUADRANT, :].bitcast(I32)
+                source = x_scales[z, r : 16 : SCALE_ROWS, :].bitcast(I32)
+                if r == 0 and z == 0:
+                    nc.sync.dma_start(rows[:3], source[:3])
+                    nc.sync.dma_start(rows[3:], source[3:])
+                else:
+                    nc.sync.dma_start(rows, source)
 
         load_scale_rows(0)
         load_scale_rows(1)
@@ -190,7 +193,8 @@ def tile_picked_edgeup_silu_p_kernel(
 
         def store(c):
             staged = sb(f"res{c}", [P, CHUNK], F32)
-            nc.vector.tensor_copy(staged[:], results[c][:])
+            copy = nc.scalar.copy if c >= 2 else nc.vector.tensor_copy
+            copy(staged[:], results[c][:])
             nc.sync.dma_start(out[:, c * CHUNK : (c + 1) * CHUNK], staged[:])
 
         values = [cast_edges(0), cast_edges(1)]

@@ -24,6 +24,8 @@ CHUNKS = V // CHUNK
 
 SCALAR_SHARE_W1 = (128, 80)
 SCALAR_SHARE_W2 = (96, 72)
+STAGE_FIRST = (11, 15)
+STAGE_STEP = 7
 EDGE_LOADS = ((0, 2), (2, 1), (3, 1))
 
 
@@ -42,6 +44,9 @@ def tile_picked_edgeup_silu_p_kernel(
         nc.gpsimd.memset(xs_all[:].bitcast(I32), 0)
         w4s = sb("w4s", [P, N], U8)
         nc.vector.memset(w4s[:].bitcast(I32), 0)
+        planes = [sb(f"plane{z}", [P, S], U8) for z in range(2)]
+        for plane in planes:
+            nc.vector.memset(plane[:].bitcast(I32), 0)
 
         def load_rows(name, rows):
             raw = sb(name, [P, PACK, rows.shape[1]], F32)
@@ -53,27 +58,30 @@ def tile_picked_edgeup_silu_p_kernel(
             nc.sync.dma_start(tile[:], words.rearrange("p n t -> p (n t)").bitcast(I32))
             return tile
 
-        xw0 = load_words("xw0", x_words[0])
+        raw_w10 = load_rows("raw_w10", w1[0:K_PASS, :])
         offsets = sb("offsets", [P, S // 16], U16)
         nc.sync.dma_start(offsets[:], offs)
-        def load_scale_rows(r):
-            for z in range(2):
-                rows = xs_all[SCALE_ROWS * z + r : P : QUADRANT, :].bitcast(I32)
-                source = x_scales[z, r : 16 : SCALE_ROWS, :].bitcast(I32)
-                if r == 0 and z == 0:
-                    nc.sync.dma_start(rows[:3], source[:3])
-                    nc.sync.dma_start(rows[3:], source[3:])
-                else:
-                    nc.sync.dma_start(rows, source)
+        for z in range(2):
+            rows = xs_all[STAGE_FIRST[z] : STAGE_FIRST[z] + 16 * STAGE_STEP - STAGE_STEP + 1 : STAGE_STEP, :]
+            nc.sync.dma_start(rows.bitcast(I32), x_scales[z].bitcast(I32))
+        xs = sb("xs", [P, S], U8)
+        nc.vector.tensor_copy(xs[:], xs_all[:].indirect(offsets[:]))
 
-        load_scale_rows(0)
-        load_scale_rows(1)
-        raw_w10 = load_rows("raw_w10", w1[0:K_PASS, :])
-        load_scale_rows(2)
-        load_scale_rows(3)
+        def place_scale_rows(z):
+            for r in range(SCALE_ROWS):
+                first = STAGE_FIRST[z] + STAGE_STEP * r
+                step = STAGE_STEP * SCALE_ROWS
+                nc.sync.dma_start(
+                    planes[z][SCALE_ROWS * z + r : P : QUADRANT, :].bitcast(I32),
+                    xs[first : first + 3 * step + 1 : step, :].bitcast(I32),
+                )
+
+        xw0 = load_words("xw0", x_words[0])
         xw1 = load_words("xw1", x_words[1])
         raw_w20 = load_rows("raw_w20", w2[0:K_PASS, :])
+        place_scale_rows(0)
         raw_w11 = load_rows("raw_w11", w1[K_PASS:K, :])
+        place_scale_rows(1)
         raw_w21 = load_rows("raw_w21", w2[K_PASS:K, :])
         raw_w3 = load_rows("raw_w3", w3)
         raw_e = []
@@ -138,16 +146,14 @@ def tile_picked_edgeup_silu_p_kernel(
                 chunk_pass(weights, c, words[:, cols], scales[SCALE_ROWS * z :, cols], opens, False)
 
         xg0 = gather_words("xg0", xw0)
-        xs = sb("xs", [P, S], U8)
-        nc.vector.tensor_copy(xs[:], xs_all[:].indirect(offsets[:]))
         unread = sb("unread", [P, 1], F32)
         nc.scalar.activation(unread[:], raw_w10[:, 0, 0:1], SILU)
         dealt_w10 = cast_weights("g10", raw_w10, SCALAR_SHARE_W1[0])
         xg1 = gather_words("xg1", xw1)
-        node_pass(quantise("q10", dealt_w10), xg0, xs, 0, 0, True)
-        node_pass(quantise("q20", cast_weights("g20", raw_w20, SCALAR_SHARE_W2[0])), xg0, xs, 0, 1, False)
-        node_pass(quantise("q11", cast_weights("g11", raw_w11, SCALAR_SHARE_W1[1])), xg1, xs, 1, 0, False)
-        node_pass(quantise("q21", cast_weights("g21", raw_w21, SCALAR_SHARE_W2[1])), xg1, xs, 1, 1, False)
+        node_pass(quantise("q10", dealt_w10), xg0, planes[0], 0, 0, True)
+        node_pass(quantise("q20", cast_weights("g20", raw_w20, SCALAR_SHARE_W2[0])), xg0, planes[0], 0, 1, False)
+        node_pass(quantise("q11", cast_weights("g11", raw_w11, SCALAR_SHARE_W1[1])), xg1, planes[1], 1, 0, False)
+        node_pass(quantise("q21", cast_weights("g21", raw_w21, SCALAR_SHARE_W2[1])), xg1, planes[1], 1, 1, False)
 
         q3 = operand("q3", H)
         src3 = raw_w3[:].rearrange("p j (m u e) -> p u m j e", u=2, e=2)

@@ -21,6 +21,7 @@ QUADRANT = 32
 SCALE_ROWS = 4
 CHUNK = 128
 CHUNKS = V // CHUNK
+HALF = CHUNK // 2
 
 SCALAR_SHARE_W1 = (128, 80)
 SCALAR_SHARE_W2 = (96, 72)
@@ -172,23 +173,28 @@ def tile_picked_edgeup_silu_p_kernel(
             )
             return values
 
-        def first_layer(c, edge_values):
+        def close_chunk(c, edge_values):
             words, scales = quantise(f"qe{c}", edge_values)
             chunk_pass(q3, c, words[:], scales[:], False, True)
-            hidden = sb(f"hb{c}", [P, PACK * CHUNK], BF16)
+
+        def silu(name, c, first, edges):
+            hidden = sb(name, [P, PACK * edges], BF16)
             nc.scalar.activation(
                 hidden[:].rearrange("p (v t) -> p v t", t=PACK),
-                banks[c][:].rearrange("p t v -> p v t"),
+                banks[c][:, :, first : first + edges].rearrange("p t v -> p v t"),
                 SILU,
             )
             return hidden
 
-        results = [psum.tile([P, CHUNK], F32, name=f"o{c}") for c in range(CHUNKS)]
+        def first_layer(c, edge_values):
+            close_chunk(c, edge_values)
+            return silu(f"hb{c}", c, 0, CHUNK)
 
-        def second_layer(c, hidden):
-            words, scales = quantise(f"qh{c}", hidden)
+        def second_layer(name, hidden, bank):
+            words, scales = quantise(name, hidden)
+            result = psum.tile([P, words.shape[1]], F32, name=name + "_o", tag=bank)
             nc.tensor.matmul_mx(
-                out=results[c][:],
+                out=result[:],
                 lhsT=w4w[:].bitcast(FP8X4),
                 lhsT_scale=w4s[:],
                 rhs=words[:].bitcast(FP8X4),
@@ -196,11 +202,11 @@ def tile_picked_edgeup_silu_p_kernel(
                 start=True,
                 stop=True,
             )
+            return result
 
-        def store(c):
+        def store(c, copy, result):
             staged = sb(f"res{c}", [P, CHUNK], F32)
-            copy = nc.scalar.copy if c >= 2 else nc.vector.tensor_copy
-            copy(staged[:], results[c][:])
+            copy(staged[:], result[:])
             nc.sync.dma_start(out[:, c * CHUNK : (c + 1) * CHUNK], staged[:])
 
         values = [cast_edges(0), cast_edges(1)]
@@ -209,9 +215,16 @@ def tile_picked_edgeup_silu_p_kernel(
         values.append(cast_edges(2))
         hidden.append(first_layer(1, values[1]))
         hidden.append(first_layer(2, values[2]))
-        hidden.append(first_layer(3, cast_edges(3)))
-        second_layer(0, hidden[0])
-        for c in range(1, CHUNKS):
-            second_layer(c, hidden[c])
-            store(c - 1)
-        store(CHUNKS - 1)
+        close_chunk(3, cast_edges(3))
+        halves = [silu(f"hb3{i}", 3, i * HALF, HALF) for i in range(2)]
+        result0 = second_layer("qh0", hidden[0], "o0")
+        result1 = second_layer("qh1", hidden[1], "o1")
+        store(0, nc.vector.tensor_copy, result0)
+        result2 = second_layer("qh2", hidden[2], "o2")
+        store(1, nc.vector.tensor_copy, result1)
+        result3 = [second_layer(f"qh3{i}", halves[i], ("o3", "o0")[i]) for i in range(2)]
+        store(2, nc.scalar.copy, result2)
+        staged = sb("res3", [P, CHUNK], F32)
+        for i in range(2):
+            nc.scalar.copy(staged[:, i * HALF : (i + 1) * HALF], result3[i][:])
+        nc.sync.dma_start(out[:, 3 * CHUNK :], staged[:])

@@ -89,7 +89,10 @@ def tile_picked_edgeup_silu_p_kernel(
         for first, count in EDGE_LOADS:
             raw = load_rows(f"raw_e{first}", eT[:, first * CHUNK : (first + count) * CHUNK])
             raw_e.extend(raw[:, :, i * CHUNK : (i + 1) * CHUNK] for i in range(count))
-        w4w = load_words("w4w", w4_words[0])
+        w4w = sb("w4w", [P, N], I32)
+        w4_rows = w4_words[0].rearrange("p n t -> p (n t)").bitcast(I32)
+        for a, b in ((0, 64), (64, 96), (96, 128)):
+            nc.sync.dma_start(w4w[:, a:b], w4_rows[:, a:b])
         for q in range(4):
             nc.sync.dma_start(
                 w4s[QUADRANT * q : QUADRANT * q + SCALE_ROWS, :].bitcast(I32),

@@ -20,8 +20,8 @@ K_PASS = P * PACK
 QUADRANT = 32
 SCALE_ROWS = 4
 CHUNK = 128
-CHUNKS = V // CHUNK
 HALF = CHUNK // 2
+WINDOWS = (0, 128, 256, 320, 384)
 
 SCALAR_SHARE_W1 = (128, 80)
 SCALAR_SHARE_W2 = (96, 72)
@@ -38,8 +38,8 @@ def tile_picked_edgeup_silu_p_kernel(
         keep = ctx.enter_context(tc.tile_pool(name="keep", bufs=1))
         psum = ctx.enter_context(tc.psum_pool(name="psum", bufs=1))
 
-        def sb(name, shape, dtype):
-            return keep.tile(shape, dtype, name=name, align_bytes=64)
+        def sb(name, shape, dtype, tag=None):
+            return keep.tile(shape, dtype, name=name, tag=tag or name, align_bytes=64)
 
         xs_all = sb("xs_all", [P, T], U8)
         nc.gpsimd.memset(xs_all[:].bitcast(I32), 0)
@@ -89,15 +89,15 @@ def tile_picked_edgeup_silu_p_kernel(
         for first, count in EDGE_LOADS:
             raw = load_rows(f"raw_e{first}", eT[:, first * CHUNK : (first + count) * CHUNK])
             raw_e.extend(raw[:, :, i * CHUNK : (i + 1) * CHUNK] for i in range(count))
-        w4w = sb("w4w", [P, N], I32)
-        w4_rows = w4_words[0].rearrange("p n t -> p (n t)").bitcast(I32)
-        for a, b in ((0, 64), (64, 96), (96, 128)):
-            nc.sync.dma_start(w4w[:, a:b], w4_rows[:, a:b])
         for q in range(4):
             nc.sync.dma_start(
                 w4s[QUADRANT * q : QUADRANT * q + SCALE_ROWS, :].bitcast(I32),
                 w4_scales[0, SCALE_ROWS * q : SCALE_ROWS * (q + 1), :].bitcast(I32),
             )
+        w4w = sb("w4w", [P, N], I32)
+        w4_rows = w4_words[0].rearrange("p n t -> p (n t)").bitcast(I32)
+        for a, b in ((0, 64), (64, 96), (96, 128)):
+            nc.sync.dma_start(w4w[a:b, :], w4_rows[a:b, :])
 
         def cast_weights(name, raw, m_scalar):
             dealt = sb(name, [P, PACK * H], BF16)
@@ -108,8 +108,8 @@ def tile_picked_edgeup_silu_p_kernel(
                 nc.vector.tensor_copy(dst[:, :, m_scalar:], src[:, :, m_scalar:])
             return dealt
 
-        def operand(name, width):
-            return sb(name + "_c", [P, width], U32), sb(name + "_s", [P, width], U8)
+        def operand(name, width, tag=None):
+            return sb(name + "_c", [P, width], U32, tag), sb(name + "_s", [P, width], U8)
 
         def quantise_into(mx, first, values):
             width = values.shape[1] // PACK
@@ -129,13 +129,13 @@ def tile_picked_edgeup_silu_p_kernel(
             nc.vector.tensor_copy(picked[:], table[:].bitcast(U32).indirect(offsets[:]))
             return picked
 
-        banks = [psum.tile([P, PACK, CHUNK], F32, name=f"h{c}") for c in range(CHUNKS)]
+        banks = [psum.tile([P, PACK, CHUNK], F32, name=f"h{b}", tag=f"h{b}") for b in range(len(WINDOWS))]
 
-        def chunk_pass(weights, c, words, scales, opens, closes):
+        def bank_pass(weights, b, words, scales, opens, closes):
             for t in range(PACK):
                 cols = slice(t * P, (t + 1) * P)
                 nc.tensor.matmul_mx(
-                    out=banks[c][:, t, :],
+                    out=banks[b][:, t, :],
                     lhsT=weights[0][:, cols].bitcast(FP8X4),
                     lhsT_scale=weights[1][:, cols],
                     rhs=words.bitcast(FP8X4),
@@ -145,9 +145,9 @@ def tile_picked_edgeup_silu_p_kernel(
                 )
 
         def node_pass(weights, words, scales, z, side, opens):
-            for c in range(CHUNKS):
-                cols = slice(side * V + c * CHUNK, side * V + (c + 1) * CHUNK)
-                chunk_pass(weights, c, words[:, cols], scales[SCALE_ROWS * z :, cols], opens, False)
+            for b, first in enumerate(WINDOWS):
+                cols = slice(side * V + first, side * V + first + CHUNK)
+                bank_pass(weights, b, words[:, cols], scales[SCALE_ROWS * z :, cols], opens, False)
 
         xg0 = gather_words("xg0", xw0)
         unread = sb("unread", [P, 1], F32)
@@ -167,67 +167,79 @@ def tile_picked_edgeup_silu_p_kernel(
         nc.vector.tensor_copy(dst3[1], src3[:, 1])
         quantise_into(q3, 2 * P, dealt_w3[1][:])
 
-        def cast_edges(c):
-            values = sb(f"ge{c}", [P, PACK * CHUNK], BF16)
-            copy = nc.scalar.copy if c == 1 else nc.vector.tensor_copy
+        qe = operand("qe", V)
+
+        def cast_edges(copy, values, c, first, count):
             copy(
-                values[:].rearrange("p (g i j) -> p g j i", i=4, j=PACK),
-                raw_e[c].rearrange("p j (g i) -> p g j i", i=4),
+                values[:, PACK * first : PACK * (first + count)].rearrange("p (g i j) -> p g j i", i=4, j=PACK),
+                raw_e[c][:, :, first : first + count].rearrange("p j (g i) -> p g j i", i=4),
             )
-            return values
 
-        def close_chunk(c, edge_values):
-            words, scales = quantise(f"qe{c}", edge_values)
-            chunk_pass(q3, c, words[:], scales[:], False, True)
+        def close_bank(b):
+            cols = slice(WINDOWS[b], WINDOWS[b] + CHUNK)
+            bank_pass(q3, b, qe[0][:, cols], qe[1][:, cols], False, True)
 
-        def silu(name, c, first, edges):
-            hidden = sb(name, [P, PACK * edges], BF16)
+        def silu(b, first):
+            hidden = sb(f"hb{b}", [P, PACK * (CHUNK - first)], BF16)
             nc.scalar.activation(
                 hidden[:].rearrange("p (v t) -> p v t", t=PACK),
-                banks[c][:, :, first : first + edges].rearrange("p t v -> p v t"),
+                banks[b][:, :, first:].rearrange("p t v -> p v t"),
                 SILU,
             )
             return hidden
 
-        def first_layer(c, edge_values):
-            close_chunk(c, edge_values)
-            return silu(f"hb{c}", c, 0, CHUNK)
-
-        def second_layer(name, hidden, bank):
-            words, scales = quantise(name, hidden)
-            result = psum.tile([P, words.shape[1]], F32, name=name + "_o", tag=bank)
+        def second_layer(name, hidden, bank, mx, first):
+            quantise_into(mx, first, hidden[:])
+            width = hidden.shape[1] // PACK
+            words, scales = (part[:, first : first + width] for part in mx)
+            result = psum.tile([P, width], F32, name=name + "_o", tag=bank)
             nc.tensor.matmul_mx(
                 out=result[:],
                 lhsT=w4w[:].bitcast(FP8X4),
                 lhsT_scale=w4s[:],
-                rhs=words[:].bitcast(FP8X4),
-                rhs_scale=scales[:],
+                rhs=words.bitcast(FP8X4),
+                rhs_scale=scales,
                 start=True,
                 stop=True,
             )
             return result
 
-        def store(c, copy, result):
-            staged = sb(f"res{c}", [P, CHUNK], F32)
-            copy(staged[:], result[:])
-            nc.sync.dma_start(out[:, c * CHUNK : (c + 1) * CHUNK], staged[:])
-
-        values = [cast_edges(0), cast_edges(1)]
+        ge0 = sb("ge0", [P, PACK * CHUNK], BF16, "ge")
+        cast_edges(nc.vector.tensor_copy, ge0, 0, 0, HALF)
+        cast_edges(nc.scalar.copy, ge0, 0, HALF, HALF)
+        ge1 = sb("ge1", [P, PACK * CHUNK], BF16)
+        cast_edges(nc.scalar.copy, ge1, 1, 0, CHUNK)
         quantise_into(q3, 0, dealt_w3[0][:])
-        hidden = [first_layer(0, values[0])]
-        values.append(cast_edges(2))
-        hidden.append(first_layer(1, values[1]))
-        hidden.append(first_layer(2, values[2]))
-        close_chunk(3, cast_edges(3))
-        halves = [silu(f"hb3{i}", 3, i * HALF, HALF) for i in range(2)]
-        result0 = second_layer("qh0", hidden[0], "o0")
-        result1 = second_layer("qh1", hidden[1], "o1")
-        store(0, nc.vector.tensor_copy, result0)
-        result2 = second_layer("qh2", hidden[2], "o2")
-        store(1, nc.vector.tensor_copy, result1)
-        result3 = [second_layer(f"qh3{i}", halves[i], ("o3", "o0")[i]) for i in range(2)]
-        store(2, nc.scalar.copy, result2)
-        staged = sb("res3", [P, CHUNK], F32)
+        quantise_into(qe, 0, ge0[:])
+        close_bank(0)
+        ge2 = sb("ge2", [P, PACK * CHUNK], BF16, "ge")
+        cast_edges(nc.vector.tensor_copy, ge2, 2, 0, HALF)
+        cast_edges(nc.scalar.copy, ge2, 2, HALF, HALF)
+        quantise_into(qe, CHUNK, ge1[:])
+        close_bank(1)
+        quantise_into(qe, 2 * CHUNK, ge2[:])
+        close_bank(2)
+        hidden = [silu(b, 0) for b in range(3)]
+        ge3 = sb("ge3", [P, PACK * CHUNK], BF16, "ge")
         for i in range(2):
-            nc.scalar.copy(staged[:, i * HALF : (i + 1) * HALF], result3[i][:])
-        nc.sync.dma_start(out[:, 3 * CHUNK :], staged[:])
+            cast_edges(nc.vector.tensor_copy, ge3, 3, i * HALF, HALF)
+        for i in range(2):
+            quantise_into(qe, 3 * CHUNK + i * HALF, ge3[:, i * PACK * HALF : (i + 1) * PACK * HALF])
+            close_bank(3 + i)
+        hidden.extend(silu(b, HALF) for b in (3, 4))
+        staged = [sb(f"res{c}", [P, CHUNK], F32) for c in range(4)]
+        qh = [operand("qh01", 2 * CHUNK, "ge"), operand("qh23", 2 * CHUNK)]
+        result = [second_layer(f"r{b}", hidden[b], f"o{b}", qh[b // 2], b % 2 * CHUNK) for b in range(3)]
+        result.append(second_layer("r3", hidden[3], "h0", qh[1], CHUNK))
+
+        def store(c, copy):
+            copy(staged[c][:], result[c][:])
+            nc.sync.dma_start(out[:, c * CHUNK : (c + 1) * CHUNK], staged[c][:])
+
+        store(0, nc.vector.tensor_copy)
+        result.append(second_layer("r4", hidden[4], "h1", qh[1], CHUNK + HALF))
+        store(1, nc.scalar.copy)
+        store(2, nc.vector.tensor_copy)
+        for i in range(2):
+            nc.scalar.copy(staged[3][:, i * HALF : (i + 1) * HALF], result[3 + i][:])
+        nc.sync.dma_start(out[:, 3 * CHUNK :], staged[3][:])

@@ -82,8 +82,8 @@ def tile_picked_edgeup_silu_p_kernel(
         raw_w20 = load_rows("raw_w20", w2[0:K_PASS, :])
         place_scale_rows(0)
         raw_w11 = load_rows("raw_w11", w1[K_PASS:K, :])
-        place_scale_rows(1)
         raw_w21 = load_rows("raw_w21", w2[K_PASS:K, :])
+        place_scale_rows(1)
         raw_w3 = load_rows("raw_w3", w3)
         raw_e = []
         for first, count in EDGE_LOADS:
@@ -204,17 +204,15 @@ def tile_picked_edgeup_silu_p_kernel(
             )
             return result
 
-        ge0 = sb("ge0", [P, PACK * CHUNK], BF16, "ge")
-        cast_edges(nc.vector.tensor_copy, ge0, 0, 0, HALF)
-        cast_edges(nc.scalar.copy, ge0, 0, HALF, HALF)
+        ge0 = sb("ge0", [P, PACK * CHUNK], BF16)
+        cast_edges(nc.vector.tensor_copy, ge0, 0, 0, CHUNK)
         ge1 = sb("ge1", [P, PACK * CHUNK], BF16)
         cast_edges(nc.scalar.copy, ge1, 1, 0, CHUNK)
         quantise_into(q3, 0, dealt_w3[0][:])
         quantise_into(qe, 0, ge0[:])
         close_bank(0)
-        ge2 = sb("ge2", [P, PACK * CHUNK], BF16, "ge")
-        cast_edges(nc.vector.tensor_copy, ge2, 2, 0, HALF)
-        cast_edges(nc.scalar.copy, ge2, 2, HALF, HALF)
+        ge2 = sb("ge2", [P, PACK * CHUNK], BF16)
+        cast_edges(nc.vector.tensor_copy, ge2, 2, 0, CHUNK)
         quantise_into(qe, CHUNK, ge1[:])
         close_bank(1)
         quantise_into(qe, 2 * CHUNK, ge2[:])

@@ -24,7 +24,7 @@ HALF = CHUNK // 2
 WINDOWS = (0, 128, 256, 320, 384)
 
 SCALAR_SHARE_W1 = (128, 80)
-SCALAR_SHARE_W2 = (96, 72)
+SCALAR_SHARE_W2 = 96
 STAGE_FIRST = (11, 15)
 STAGE_STEP = 7
 EDGE_LOADS = ((0, 2), (2, 1), (3, 1))
@@ -155,16 +155,25 @@ def tile_picked_edgeup_silu_p_kernel(
         dealt_w10 = cast_weights("g10", raw_w10, SCALAR_SHARE_W1[0])
         xg1 = gather_words("xg1", xw1)
         node_pass(quantise("q10", dealt_w10), xg0, planes[0], 0, 0, True)
-        node_pass(quantise("q20", cast_weights("g20", raw_w20, SCALAR_SHARE_W2[0])), xg0, planes[0], 0, 1, False)
+        node_pass(quantise("q20", cast_weights("g20", raw_w20, SCALAR_SHARE_W2)), xg0, planes[0], 0, 1, False)
         node_pass(quantise("q11", cast_weights("g11", raw_w11, SCALAR_SHARE_W1[1])), xg1, planes[1], 1, 0, False)
-        node_pass(quantise("q21", cast_weights("g21", raw_w21, SCALAR_SHARE_W2[1])), xg1, planes[1], 1, 1, False)
+
+        def cast_pairs(name, raw):
+            src = raw[:].rearrange("p j (m u e) -> p u m j e", u=2, e=2)
+            dealt = [sb(f"{name}{u}", [P, 2 * H], BF16) for u in range(2)]
+            dst = [pair[:].rearrange("p (e m j) -> p m j e", e=2, j=PACK) for pair in dealt]
+            nc.scalar.copy(dst[0], src[:, 0])
+            nc.vector.tensor_copy(dst[1], src[:, 1])
+            return dealt
+
+        q21 = operand("q21", H)
+        dealt_w21 = cast_pairs("g21", raw_w21)
+        quantise_into(q21, 2 * P, dealt_w21[1][:])
+        quantise_into(q21, 0, dealt_w21[0][:])
+        node_pass(q21, xg1, planes[1], 1, 1, False)
 
         q3 = operand("q3", H)
-        src3 = raw_w3[:].rearrange("p j (m u e) -> p u m j e", u=2, e=2)
-        dealt_w3 = [sb(f"g3{u}", [P, 2 * H], BF16) for u in range(2)]
-        dst3 = [pair[:].rearrange("p (e m j) -> p m j e", e=2, j=PACK) for pair in dealt_w3]
-        nc.scalar.copy(dst3[0], src3[:, 0])
-        nc.vector.tensor_copy(dst3[1], src3[:, 1])
+        dealt_w3 = cast_pairs("g3", raw_w3)
         quantise_into(q3, 2 * P, dealt_w3[1][:])
 
         qe = operand("qe", V)

@@ -25,8 +25,7 @@ WINDOWS = (0, 128, 256, 320, 384)
 
 SCALAR_SHARE_W1 = (128, 80)
 SCALAR_SHARE_W2 = 96
-STAGE_FIRST = (11, 15)
-STAGE_STEP = 7
+STAGE_STEP = 8
 EDGE_LOADS = ((0, 2), (2, 1), (3, 1))
 
 
@@ -45,9 +44,6 @@ def tile_picked_edgeup_silu_p_kernel(
         nc.gpsimd.memset(xs_all[:].bitcast(I32), 0)
         w4s = sb("w4s", [P, N], U8)
         nc.vector.memset(w4s[:].bitcast(I32), 0)
-        planes = [sb(f"plane{z}", [P, S], U8) for z in range(2)]
-        for plane in planes:
-            nc.vector.memset(plane[:].bitcast(I32), 0)
 
         def load_rows(name, rows):
             raw = sb(name, [P, PACK, rows.shape[1]], F32)
@@ -63,40 +59,42 @@ def tile_picked_edgeup_silu_p_kernel(
         offsets = sb("offsets", [P, S // 16], U16)
         nc.sync.dma_start(offsets[:], offs)
         for z in range(2):
-            rows = xs_all[STAGE_FIRST[z] : STAGE_FIRST[z] + 16 * STAGE_STEP - STAGE_STEP + 1 : STAGE_STEP, :]
+            rows = xs_all[SCALE_ROWS * z : P : STAGE_STEP, :]
             nc.sync.dma_start(rows.bitcast(I32), x_scales[z].bitcast(I32))
         xs = sb("xs", [P, S], U8)
         nc.vector.tensor_copy(xs[:], xs_all[:].indirect(offsets[:]))
+        plane = sb("plane", [P, S], U8)
+        nc.vector.tensor_copy(plane[:].bitcast(I32), xs[:].bitcast(I32))
 
-        def place_scale_rows(z):
-            for r in range(SCALE_ROWS):
-                first = STAGE_FIRST[z] + STAGE_STEP * r
-                step = STAGE_STEP * SCALE_ROWS
-                nc.sync.dma_start(
-                    planes[z][SCALE_ROWS * z + r : P : QUADRANT, :].bitcast(I32),
-                    xs[first : first + 3 * step + 1 : step, :].bitcast(I32),
-                )
+        def load_w4_scales(q):
+            nc.sync.dma_start(
+                w4s[QUADRANT * q : QUADRANT * q + SCALE_ROWS, :].bitcast(I32),
+                w4_scales[0, SCALE_ROWS * q : SCALE_ROWS * (q + 1), :].bitcast(I32),
+            )
 
         xw0 = load_words("xw0", x_words[0])
         xw1 = load_words("xw1", x_words[1])
         raw_w20 = load_rows("raw_w20", w2[0:K_PASS, :])
-        place_scale_rows(0)
+        for r in range(1, SCALE_ROWS):
+            for z in range(2):
+                nc.sync.dma_start(
+                    plane[SCALE_ROWS * z + r : P : QUADRANT, :].bitcast(I32),
+                    xs[SCALE_ROWS * z + STAGE_STEP * r : P : QUADRANT, :].bitcast(I32),
+                )
         raw_w11 = load_rows("raw_w11", w1[K_PASS:K, :])
         raw_w21 = load_rows("raw_w21", w2[K_PASS:K, :])
-        place_scale_rows(1)
+        load_w4_scales(0)
+        load_w4_scales(1)
         raw_w3 = load_rows("raw_w3", w3)
         raw_e = []
         for first, count in EDGE_LOADS:
             raw = load_rows(f"raw_e{first}", eT[:, first * CHUNK : (first + count) * CHUNK])
             raw_e.extend(raw[:, :, i * CHUNK : (i + 1) * CHUNK] for i in range(count))
-        for q in range(4):
-            nc.sync.dma_start(
-                w4s[QUADRANT * q : QUADRANT * q + SCALE_ROWS, :].bitcast(I32),
-                w4_scales[0, SCALE_ROWS * q : SCALE_ROWS * (q + 1), :].bitcast(I32),
-            )
+        load_w4_scales(2)
+        load_w4_scales(3)
         w4w = sb("w4w", [P, N], I32)
         w4_rows = w4_words[0].rearrange("p n t -> p (n t)").bitcast(I32)
-        for a, b in ((0, 64), (64, 96), (96, 128)):
+        for a, b in ((0, 32), (32, 64), (64, 96), (96, 112), (112, 128)):
             nc.sync.dma_start(w4w[a:b, :], w4_rows[a:b, :])
 
         def cast_weights(name, raw, m_scalar):
@@ -154,9 +152,9 @@ def tile_picked_edgeup_silu_p_kernel(
         nc.scalar.activation(unread[:], raw_w10[:, 0, 0:1], SILU)
         dealt_w10 = cast_weights("g10", raw_w10, SCALAR_SHARE_W1[0])
         xg1 = gather_words("xg1", xw1)
-        node_pass(quantise("q10", dealt_w10), xg0, planes[0], 0, 0, True)
-        node_pass(quantise("q20", cast_weights("g20", raw_w20, SCALAR_SHARE_W2)), xg0, planes[0], 0, 1, False)
-        node_pass(quantise("q11", cast_weights("g11", raw_w11, SCALAR_SHARE_W1[1])), xg1, planes[1], 1, 0, False)
+        node_pass(quantise("q10", dealt_w10), xg0, plane, 0, 0, True)
+        node_pass(quantise("q20", cast_weights("g20", raw_w20, SCALAR_SHARE_W2)), xg0, plane, 0, 1, False)
+        node_pass(quantise("q11", cast_weights("g11", raw_w11, SCALAR_SHARE_W1[1])), xg1, plane, 1, 0, False)
 
         def cast_pairs(name, raw):
             src = raw[:].rearrange("p j (m u e) -> p u m j e", u=2, e=2)
@@ -170,7 +168,7 @@ def tile_picked_edgeup_silu_p_kernel(
         dealt_w21 = cast_pairs("g21", raw_w21)
         quantise_into(q21, 2 * P, dealt_w21[1][:])
         quantise_into(q21, 0, dealt_w21[0][:])
-        node_pass(q21, xg1, planes[1], 1, 1, False)
+        node_pass(q21, xg1, plane, 1, 1, False)
 
         q3 = operand("q3", H)
         dealt_w3 = cast_pairs("g3", raw_w3)

@@ -21,7 +21,7 @@ QUADRANT = 32
 SCALE_ROWS = 4
 CHUNK = 128
 HALF = CHUNK // 2
-WINDOWS = (0, 128, 256, 320, 384)
+WINDOWS = (0, 128, 256, 384)
 
 SCALAR_SHARE_W1 = (128, 80)
 SCALAR_SHARE_W2 = 96
@@ -186,11 +186,11 @@ def tile_picked_edgeup_silu_p_kernel(
             cols = slice(WINDOWS[b], WINDOWS[b] + CHUNK)
             bank_pass(q3, b, qe[0][:, cols], qe[1][:, cols], False, True)
 
-        def silu(b, first):
-            hidden = sb(f"hb{b}", [P, PACK * (CHUNK - first)], BF16)
+        def silu(b, first, count):
+            hidden = sb(f"hb{b}_{first}", [P, PACK * count], BF16)
             nc.scalar.activation(
                 hidden[:].rearrange("p (v t) -> p v t", t=PACK),
-                banks[b][:, :, first:].rearrange("p t v -> p v t"),
+                banks[b][:, :, first : first + count].rearrange("p t v -> p v t"),
                 SILU,
             )
             return hidden
@@ -224,14 +224,12 @@ def tile_picked_edgeup_silu_p_kernel(
         close_bank(1)
         quantise_into(qe, 2 * CHUNK, ge2[:])
         close_bank(2)
-        hidden = [silu(b, 0) for b in range(3)]
+        hidden = [silu(b, 0, CHUNK) for b in range(3)]
         ge3 = sb("ge3", [P, PACK * CHUNK], BF16, "ge")
-        for i in range(2):
-            cast_edges(nc.vector.tensor_copy, ge3, 3, i * HALF, HALF)
-        for i in range(2):
-            quantise_into(qe, 3 * CHUNK + i * HALF, ge3[:, i * PACK * HALF : (i + 1) * PACK * HALF])
-            close_bank(3 + i)
-        hidden.extend(silu(b, HALF) for b in (3, 4))
+        cast_edges(nc.vector.tensor_copy, ge3, 3, 0, CHUNK)
+        quantise_into(qe, 3 * CHUNK, ge3[:])
+        close_bank(3)
+        hidden.extend(silu(3, first, HALF) for first in (0, HALF))
         staged = [sb(f"res{c}", [P, CHUNK], F32) for c in range(4)]
         qh = [operand("qh01", 2 * CHUNK, "ge"), operand("qh23", 2 * CHUNK)]
         result = [second_layer(f"r{b}", hidden[b], f"o{b}", qh[b // 2], b % 2 * CHUNK) for b in range(3)]

@@ -38,7 +38,7 @@ def tile_picked_edgeup_silu_p_kernel(
         psum = ctx.enter_context(tc.psum_pool(name="psum", bufs=1))
 
         def sb(name, shape, dtype, tag=None):
-            return keep.tile(shape, dtype, name=name, tag=tag or name, align_bytes=64)
+            return keep.tile(shape, dtype, name=name, tag=tag or name, align_bytes=256)
 
         xs_all = sb("xs_all", [P, T], U8)
         nc.gpsimd.memset(xs_all[:].bitcast(I32), 0)

@@ -26,7 +26,7 @@ WINDOWS = (0, 128, 256, 384)
 SCALAR_SHARE_W1 = (128, 80)
 SCALAR_SHARE_W2 = 96
 STAGE_STEP = 8
-EDGE_LOADS = ((0, 2), (2, 1), (3, 1))
+EDGE_LOADS = ((0, 1), (1, 1), (2, 1), (3, 1))
 
 
 def tile_picked_edgeup_silu_p_kernel(
@@ -94,7 +94,7 @@ def tile_picked_edgeup_silu_p_kernel(
         load_w4_scales(3)
         w4w = sb("w4w", [P, N], I32)
         w4_rows = w4_words[0].rearrange("p n t -> p (n t)").bitcast(I32)
-        for a, b in ((0, 32), (32, 64), (64, 96), (96, 112), (112, 128)):
+        for a, b in ((0, 32), (32, 64), (64, 96), (96, 128)):
             nc.sync.dma_start(w4w[a:b, :], w4_rows[a:b, :])
 
         def cast_weights(name, raw, m_scalar):
@@ -130,7 +130,7 @@ def tile_picked_edgeup_silu_p_kernel(
         banks = [psum.tile([P, PACK, CHUNK], F32, name=f"h{b}", tag=f"h{b}") for b in range(len(WINDOWS))]
 
         def bank_pass(weights, b, words, scales, opens, closes):
-            for t in range(PACK):
+            for n, t in enumerate((2, 3, 0, 1)):
                 cols = slice(t * P, (t + 1) * P)
                 nc.tensor.matmul_mx(
                     out=banks[b][:, t, :],
@@ -138,8 +138,8 @@ def tile_picked_edgeup_silu_p_kernel(
                     lhsT_scale=weights[1][:, cols],
                     rhs=words.bitcast(FP8X4),
                     rhs_scale=scales,
-                    start=opens and t == 0,
-                    stop=closes and t == PACK - 1,
+                    start=opens and n == 0,
+                    stop=closes and n == PACK - 1,
                 )
 
         def node_pass(weights, words, scales, z, side, opens):

@@ -26,7 +26,7 @@ WINDOWS = (0, 128, 256, 384)
 SCALAR_SHARE_W1 = (128, 80)
 SCALAR_SHARE_W2 = 96
 STAGE_STEP = 8
-EDGE_LOADS = ((0, 1), (1, 1), (2, 1), (3, 1))
+EDGE_LOADS = ((0, 128), (128, 128), (256, 128), (384, 128))
 
 
 def tile_picked_edgeup_silu_p_kernel(
@@ -86,10 +86,7 @@ def tile_picked_edgeup_silu_p_kernel(
         load_w4_scales(0)
         load_w4_scales(1)
         raw_w3 = load_rows("raw_w3", w3)
-        raw_e = []
-        for first, count in EDGE_LOADS:
-            raw = load_rows(f"raw_e{first}", eT[:, first * CHUNK : (first + count) * CHUNK])
-            raw_e.extend(raw[:, :, i * CHUNK : (i + 1) * CHUNK] for i in range(count))
+        raw_e = [load_rows(f"raw_e{first}", eT[:, first : first + count]) for first, count in EDGE_LOADS]
         load_w4_scales(2)
         load_w4_scales(3)
         w4w = sb("w4w", [P, N], I32)
@@ -176,10 +173,11 @@ def tile_picked_edgeup_silu_p_kernel(
 
         qe = operand("qe", V)
 
-        def cast_edges(copy, values, c, first, count):
+        def cast_edges(copy, values, c, first, count, source=None):
+            source = first if source is None else source
             copy(
                 values[:, PACK * first : PACK * (first + count)].rearrange("p (g i j) -> p g j i", i=4, j=PACK),
-                raw_e[c][:, :, first : first + count].rearrange("p j (g i) -> p g j i", i=4),
+                raw_e[c][:, :, source : source + count].rearrange("p j (g i) -> p g j i", i=4),
             )
 
         def close_bank(b):
@@ -219,19 +217,20 @@ def tile_picked_edgeup_silu_p_kernel(
         quantise_into(qe, 0, ge0[:])
         close_bank(0)
         ge2 = sb("ge2", [P, PACK * CHUNK], BF16)
-        cast_edges(nc.vector.tensor_copy, ge2, 2, 0, CHUNK)
+        cast_edges(nc.vector.tensor_copy, ge2, 2, 0, HALF)
+        cast_edges(nc.scalar.copy, ge2, 2, HALF, HALF)
         quantise_into(qe, CHUNK, ge1[:])
         close_bank(1)
+        ge3 = sb("ge3", [P, PACK * CHUNK], BF16, "raw_e256")
         quantise_into(qe, 2 * CHUNK, ge2[:])
         close_bank(2)
         hidden = [silu(b, 0, CHUNK) for b in range(3)]
-        ge3 = sb("ge3", [P, PACK * CHUNK], BF16, "ge")
         cast_edges(nc.vector.tensor_copy, ge3, 3, 0, CHUNK)
         quantise_into(qe, 3 * CHUNK, ge3[:])
         close_bank(3)
         hidden.extend(silu(3, first, HALF) for first in (0, HALF))
         staged = [sb(f"res{c}", [P, CHUNK], F32) for c in range(4)]
-        qh = [operand("qh01", 2 * CHUNK, "ge"), operand("qh23", 2 * CHUNK)]
+        qh = [operand("qh01", 2 * CHUNK, "raw_e256"), operand("qh23", 2 * CHUNK)]
         result = [second_layer(f"r{b}", hidden[b], f"o{b}", qh[b // 2], b % 2 * CHUNK) for b in range(3)]
         result.append(second_layer("r3", hidden[3], "h0", qh[1], CHUNK))
 

@@ -25,6 +25,7 @@ WINDOWS = (0, 128, 256, 384)
 
 SCALAR_SHARE_W1 = (128, 80)
 SCALAR_SHARE_W2 = 96
+VECTOR_EDGES = 64
 STAGE_STEP = 8
 EDGE_LOADS = ((0, 128), (128, 128), (256, 128), (384, 128))
 
@@ -77,7 +78,7 @@ def tile_picked_edgeup_silu_p_kernel(
         raw_w20 = load_rows("raw_w20", w2[0:K_PASS, :])
         for r in range(1, SCALE_ROWS):
             for z in range(2):
-                nc.sync.dma_start(
+                nc.scalar.dma_start(
                     plane[SCALE_ROWS * z + r : P : QUADRANT, :].bitcast(I32),
                     xs[SCALE_ROWS * z + STAGE_STEP * r : P : QUADRANT, :].bitcast(I32),
                 )
@@ -213,12 +214,12 @@ def tile_picked_edgeup_silu_p_kernel(
         cast_edges(nc.vector.tensor_copy, ge0, 0, 0, CHUNK)
         ge1 = sb("ge1", [P, PACK * CHUNK], BF16)
         cast_edges(nc.scalar.copy, ge1, 1, 0, CHUNK)
-        quantise_into(q3, 0, dealt_w3[0][:])
         quantise_into(qe, 0, ge0[:])
+        quantise_into(q3, 0, dealt_w3[0][:])
         close_bank(0)
         ge2 = sb("ge2", [P, PACK * CHUNK], BF16)
-        cast_edges(nc.vector.tensor_copy, ge2, 2, 0, HALF)
-        cast_edges(nc.scalar.copy, ge2, 2, HALF, HALF)
+        cast_edges(nc.vector.tensor_copy, ge2, 2, 0, VECTOR_EDGES)
+        cast_edges(nc.scalar.copy, ge2, 2, VECTOR_EDGES, CHUNK - VECTOR_EDGES)
         quantise_into(qe, CHUNK, ge1[:])
         close_bank(1)
         ge3 = sb("ge3", [P, PACK * CHUNK], BF16, "raw_e256")

from contextlib import ExitStack

import concourse.mybir as mybir

K, T, S, V, H, N, J = 1024, 2048, 1024, 512, 512, 128, 512
FLOPS = 2 * (2 * K + J) * H * V + 2 * H * N * V

F32 = mybir.dt.float32
BF16 = mybir.dt.bfloat16
I32 = mybir.dt.int32
U32 = mybir.dt.uint32
U16 = mybir.dt.uint16
U8 = mybir.dt.uint8
FP8X4 = mybir.dt.float8_e4m3fn_x4
SILU = mybir.ActivationFunctionType.Silu

P = 128
PACK = 4
K_PASS = P * PACK
QUADRANT = 32
SCALE_ROWS = 4
CHUNK = 128
HALF = CHUNK // 2
WINDOWS = (0, 128, 256, 384)

SCALAR_SHARE_W1 = (128, 80)
SCALAR_SHARE_W2 = 96
VECTOR_EDGES = 64
STAGE_STEP = 8
EDGE_LOADS = ((0, 128), (128, 128), (256, 128), (384, 128))


def tile_picked_edgeup_silu_p_kernel(
    tc, x_words, x_scales, eT, w1, w2, w3, w4_words, w4_scales, offs, out
):
    nc = tc.nc
    with ExitStack() as ctx:
        keep = ctx.enter_context(tc.tile_pool(name="keep", bufs=1))
        psum = ctx.enter_context(tc.psum_pool(name="psum", bufs=1))

        def sb(name, shape, dtype, tag=None):
            return keep.tile(shape, dtype, name=name, tag=tag or name, align_bytes=256)

        xs_all = sb("xs_all", [P, T], U8)
        nc.gpsimd.memset(xs_all[:].bitcast(I32), 0)
        w4s = sb("w4s", [P, N], U8)
        nc.vector.memset(w4s[:].bitcast(I32), 0)

        def load_rows(name, rows):
            raw = sb(name, [P, PACK, rows.shape[1]], F32)
            nc.sync.dma_start(raw[:], rows.rearrange("(p j) c -> p j c", j=PACK))
            return raw

        def load_words(name, words):
            tile = sb(name, [P, words.shape[1]], I32)
            nc.sync.dma_start(tile[:], words.rearrange("p n t -> p (n t)").bitcast(I32))
            return tile

        raw_w10 = load_rows("raw_w10", w1[0:K_PASS, :])
        offsets = sb("offsets", [P, S // 16], U16)
        nc.sync.dma_start(offsets[:], offs)
        for z in range(2):
            rows = xs_all[SCALE_ROWS * z : P : STAGE_STEP, :]
            nc.sync.dma_start(rows.bitcast(I32), x_scales[z].bitcast(I32))
        xs = sb("xs", [P, S], U8)
        nc.vector.tensor_copy(xs[:], xs_all[:].indirect(offsets[:]))
        plane = sb("plane", [P, S], U8)
        nc.vector.tensor_copy(plane[:].bitcast(I32), xs[:].bitcast(I32))

        def load_w4_scales(q):
            nc.sync.dma_start(
                w4s[QUADRANT * q : QUADRANT * q + SCALE_ROWS, :].bitcast(I32),
                w4_scales[0, SCALE_ROWS * q : SCALE_ROWS * (q + 1), :].bitcast(I32),
            )

        xw0 = load_words("xw0", x_words[0])
        xw1 = load_words("xw1", x_words[1])
        raw_w20 = load_rows("raw_w20", w2[0:K_PASS, :])
        for r in range(1, SCALE_ROWS):
            for z in range(2):
                nc.scalar.dma_start(
                    plane[SCALE_ROWS * z + r : P : QUADRANT, :].bitcast(I32),
                    xs[SCALE_ROWS * z + STAGE_STEP * r : P : QUADRANT, :].bitcast(I32),
                )
        raw_w11 = load_rows("raw_w11", w1[K_PASS:K, :])
        raw_w21 = load_rows("raw_w21", w2[K_PASS:K, :])
        load_w4_scales(0)
        load_w4_scales(1)
        raw_w3 = load_rows("raw_w3", w3)
        raw_e = [load_rows(f"raw_e{first}", eT[:, first : first + count]) for first, count in EDGE_LOADS]
        load_w4_scales(2)
        load_w4_scales(3)
        w4w = sb("w4w", [P, N], I32)
        w4_rows = w4_words[0].rearrange("p n t -> p (n t)").bitcast(I32)
        for a, b in ((0, 32), (32, 64), (64, 96), (96, 128)):
            nc.sync.dma_start(w4w[a:b, :], w4_rows[a:b, :])

        def cast_weights(name, raw, m_scalar):
            dealt = sb(name, [P, PACK * H], BF16)
            dst = dealt[:].rearrange("p (u e m j) -> p u m j e", u=2, e=2, j=PACK)
            src = raw[:].rearrange("p j (m u e) -> p u m j e", u=2, e=2)
            nc.scalar.copy(dst[:, :, :m_scalar], src[:, :, :m_scalar])
            if m_scalar < P:
                nc.vector.tensor_copy(dst[:, :, m_scalar:], src[:, :, m_scalar:])
            return dealt

        def operand(name, width, tag=None):
            return sb(name + "_c", [P, width], U32, tag), sb(name + "_s", [P, width], U8)

        def quantise_into(mx, first, values):
            width = values.shape[1] // PACK
            nc.vector.quantize_mx(
                out=mx[0][:, first : first + width].bitcast(FP8X4),
                scales=mx[1][:, first : first + width],
                in_=values,
            )

        def quantise(name, values):
            mx = operand(name, values.shape[1] // PACK)
            quantise_into(mx, 0, values[:])
            return mx

        def gather_words(name, table):
            picked = sb(name, [P, S], U32)
            nc.vector.tensor_copy(picked[:], table[:].bitcast(U32).indirect(offsets[:]))
            return picked

        banks = [psum.tile([P, PACK, CHUNK], F32, name=f"h{b}", tag=f"h{b}") for b in range(len(WINDOWS))]

        def bank_pass(weights, b, words, scales, opens, closes):
            for n, t in enumerate((2, 3, 0, 1)):
                cols = slice(t * P, (t + 1) * P)
                nc.tensor.matmul_mx(
                    out=banks[b][:, t, :],
                    lhsT=weights[0][:, cols].bitcast(FP8X4),
                    lhsT_scale=weights[1][:, cols],
                    rhs=words.bitcast(FP8X4),
                    rhs_scale=scales,
                    start=opens and n == 0,
                    stop=closes and n == PACK - 1,
                )

        def node_pass(weights, words, scales, z, side, opens):
            for b, first in enumerate(WINDOWS):
                cols = slice(side * V + first, side * V + first + CHUNK)
                bank_pass(weights, b, words[:, cols], scales[SCALE_ROWS * z :, cols], opens, False)

        xg0 = gather_words("xg0", xw0)
        unread = sb("unread", [P, 1], F32)
        nc.scalar.activation(unread[:], raw_w10[:, 0, 0:1], SILU)
        dealt_w10 = cast_weights("g10", raw_w10, SCALAR_SHARE_W1[0])
        xg1 = gather_words("xg1", xw1)
        node_pass(quantise("q10", dealt_w10), xg0, plane, 0, 0, True)
        node_pass(quantise("q20", cast_weights("g20", raw_w20, SCALAR_SHARE_W2)), xg0, plane, 0, 1, False)
        node_pass(quantise("q11", cast_weights("g11", raw_w11, SCALAR_SHARE_W1[1])), xg1, plane, 1, 0, False)

        def cast_pairs(name, raw):
            src = raw[:].rearrange("p j (m u e) -> p u m j e", u=2, e=2)
            dealt = [sb(f"{name}{u}", [P, 2 * H], BF16) for u in range(2)]
            dst = [pair[:].rearrange("p (e m j) -> p m j e", e=2, j=PACK) for pair in dealt]
            nc.scalar.copy(dst[0], src[:, 0])
            nc.vector.tensor_copy(dst[1], src[:, 1])
            return dealt

        q21 = operand("q21", H)
        dealt_w21 = cast_pairs("g21", raw_w21)
        quantise_into(q21, 2 * P, dealt_w21[1][:])
        quantise_into(q21, 0, dealt_w21[0][:])
        node_pass(q21, xg1, plane, 1, 1, False)

        q3 = operand("q3", H)
        dealt_w3 = cast_pairs("g3", raw_w3)
        quantise_into(q3, 2 * P, dealt_w3[1][:])

        qe = operand("qe", V)

        def cast_edges(copy, values, c, first, count, source=None):
            source = first if source is None else source
            copy(
                values[:, PACK * first : PACK * (first + count)].rearrange("p (g i j) -> p g j i", i=4, j=PACK),
                raw_e[c][:, :, source : source + count].rearrange("p j (g i) -> p g j i", i=4),
            )

        def close_bank(b):
            cols = slice(WINDOWS[b], WINDOWS[b] + CHUNK)
            bank_pass(q3, b, qe[0][:, cols], qe[1][:, cols], False, True)

        def silu(b, first, count):
            hidden = sb(f"hb{b}_{first}", [P, PACK * count], BF16)
            nc.scalar.activation(
                hidden[:].rearrange("p (v t) -> p v t", t=PACK),
                banks[b][:, :, first : first + count].rearrange("p t v -> p v t"),
                SILU,
            )
            return hidden

        def second_layer(name, hidden, bank, mx, first):
            quantise_into(mx, first, hidden[:])
            width = hidden.shape[1] // PACK
            words, scales = (part[:, first : first + width] for part in mx)
            result = psum.tile([P, width], F32, name=name + "_o", tag=bank)
            nc.tensor.matmul_mx(
                out=result[:],
                lhsT=w4w[:].bitcast(FP8X4),
                lhsT_scale=w4s[:],
                rhs=words.bitcast(FP8X4),
                rhs_scale=scales,
                start=True,
                stop=True,
            )
            return result

        ge0 = sb("ge0", [P, PACK * CHUNK], BF16)
        cast_edges(nc.vector.tensor_copy, ge0, 0, 0, CHUNK)
        ge1 = sb("ge1", [P, PACK * CHUNK], BF16)
        cast_edges(nc.scalar.copy, ge1, 1, 0, CHUNK)
        quantise_into(qe, 0, ge0[:])
        quantise_into(q3, 0, dealt_w3[0][:])
        close_bank(0)
        ge2 = sb("ge2", [P, PACK * CHUNK], BF16)
        cast_edges(nc.vector.tensor_copy, ge2, 2, 0, VECTOR_EDGES)
        cast_edges(nc.scalar.copy, ge2, 2, VECTOR_EDGES, CHUNK - VECTOR_EDGES)
        quantise_into(qe, CHUNK, ge1[:])
        close_bank(1)
        ge3 = sb("ge3", [P, PACK * CHUNK], BF16, "raw_e256")
        quantise_into(qe, 2 * CHUNK, ge2[:])
        close_bank(2)
        hidden = [silu(b, 0, CHUNK) for b in range(3)]
        cast_edges(nc.vector.tensor_copy, ge3, 3, 0, CHUNK)
        quantise_into(qe, 3 * CHUNK, ge3[:])
        close_bank(3)
        hidden.extend(silu(3, first, HALF) for first in (0, HALF))
        staged = [sb(f"res{c}", [P, CHUNK], F32) for c in range(4)]
        qh = [operand("qh01", 2 * CHUNK, "raw_e256"), operand("qh23", 2 * CHUNK)]
        result = [second_layer(f"r{b}", hidden[b], f"o{b}", qh[b // 2], b % 2 * CHUNK) for b in range(3)]
        result.append(second_layer("r3", hidden[3], "h0", qh[1], CHUNK))

        def store(c, copy):
            copy(staged[c][:], result[c][:])
            nc.sync.dma_start(out[:, c * CHUNK : (c + 1) * CHUNK], staged[c][:])

        store(0, nc.vector.tensor_copy)
        result.append(second_layer("r4", hidden[4], "h1", qh[1], CHUNK + HALF))
        store(1, nc.scalar.copy)
        store(2, nc.vector.tensor_copy)
        for i in range(2):
            nc.scalar.copy(staged[3][:, i * HALF : (i + 1) * HALF], result[3 + i][:])
        nc.sync.dma_start(out[:, 3 * CHUNK :], staged[3][:])
